import numpy as np, ml_dtypes
CORES = [16,18,20,22]
N = 4
import mx_ref
BF = ml_dtypes.bfloat16
def gentries(a):
    return np.ascontiguousarray(a.reshape(8, 16, -1).transpose(0, 2, 1)).reshape(8, -1)
def gtable(e):
    e = np.asarray(e); return np.ascontiguousarray(e.reshape(8, -1, 16).transpose(0, 2, 1)).reshape(128, -1).astype(np.int32)
def gcols(t, e):
    v = np.concatenate([t.reshape(8, 16, -1, 4), np.zeros((8, 16, 1, 4), BF)], axis=2)
    return np.ascontiguousarray(np.stack([v[g][:, e[g]] for g in range(8)])).reshape(128, -1)
def tile(rs):
    return np.stack(rs, axis=2).reshape(128, -1).astype(BF)
def pick(q, e):
    c = np.concatenate([q[0].reshape(128, -1, 4), np.zeros((128, 1, 4), np.uint8)], axis=1); s = np.concatenate([q[1], np.ones((16, 1), np.uint8)], axis=1)
    return (np.ascontiguousarray(c[:, e].reshape(128, -1)), np.ascontiguousarray(s[:, e]))
def join(*qs):
    return (np.concatenate([q[0] for q in qs], axis=1), np.concatenate([q[1] for q in qs], axis=1))
def put(q, e, v):
    c, s = q[0].reshape(128, -1, 4).copy(), q[1].copy(); c[:, e] = v[0].reshape(128, -1, 4); s[:, e] = v[1]
    return (c.reshape(128, -1), s)
def pk(c, s):
    return (np.ascontiguousarray(c), mx_ref.live(s))
def emit(q):
    return q[0], q[1]
def packed(v, rng):
    q = [mx_ref.quantize(np.ascontiguousarray(v[r])) for r in range(N)]
    return np.stack([a for a, b in q]), np.stack([mx_ref.plane(b, rng) for a, b in q])
def values_of_codes():
    e, c = np.zeros((128, 128, 4), np.float32), np.zeros((128, 2, 4), np.uint8)
    e[np.arange(128), np.arange(128), 0] = 1
    c[:127, :, 0] = np.arange(256).reshape(2, 128).T[:127]
    return mx_ref.matmul(mx_ref.quantize(e.reshape(128, 512).astype(BF)), (c.reshape(128, 8), np.full((16, 2), 127, np.uint8))).T.reshape(-1).astype(np.float64)
CODE_VALUE, SCALE_VALUE = values_of_codes(), 2.0 ** (np.arange(256) - 127.0)
def decode(q):
    return (CODE_VALUE[q[0]].reshape(16, 8, -1, 4) * SCALE_VALUE[q[1]][:, None, :, None] + 0.0).reshape(128, -1).astype(np.float32)
def f(rng, *shape):
    return mx_ref.flush((rng.standard_normal(shape, dtype=np.float32) * np.exp2(rng.integers(-2, 3, shape[:-1] + (1,)))).astype(BF))
def wide(rng, *shape, cols=0):
    v = rng.standard_normal(shape, dtype=np.float32) * np.exp2(rng.integers(-12, 13, shape)).astype(np.float32)
    if cols: v *= np.repeat(np.exp2(rng.integers(-cols, cols + 1, shape[:-2] + (1, shape[-1] // 4))) * (rng.random(shape[:-2] + (1, shape[-1] // 4)) > 0.0625), 4, axis=-1).astype(np.float32)
    return mx_ref.flush(v.astype(BF))
T, C = 384, 96
def big(v):
    v = v.astype(np.float32)
    v[np.abs(v) < np.float32(2.0 ** -16)] = 0
    return v.astype(BF)
def numbers_of(rng):
    return {"x": np.array(f(rng, N, 128, 4 * T)), "k": np.array(f(rng, N, 128, 4 * C)), "u": np.array(f(rng, N, 128, 512)), "v": np.array(f(rng, N, 128, 512))}
def pointers(rng):
    return {"pt": np.stack([gtable(rng.integers(0, C, (8, T))) for r in range(N)]), "ad": np.stack([gtable(rng.integers(0, C, (8, C))) for r in range(N)])}
def weights(rng, still=[]):
    c = np.arange(512)
    free, hold = c[~np.isin(c // 4 % 16, still)], c[np.isin(c % 16, still)]
    m = np.zeros((N, 512, 512), np.float32)
    if len(free):
        for r in range(N): m[r, free[rng.integers(0, len(free), (12, 512))], c] = (0.5 + 1.5 * rng.random((12, 512))) * rng.choice([-1.0, 1.0], (12, 512))
    m[:, :, hold] = 0
    m[:, 4 * (hold % 128) + hold // 128, hold] = 32
    a, s = packed(m.reshape(N, 128, 4, 512).transpose(0, 1, 3, 2).reshape(N, 128, 2048).astype(BF), rng)
    return {"wc": a, "ws": s}
def setup_inputs(rng):
    return {**numbers_of(rng), **pointers(rng), **weights(rng)}
def setup_inputs_ties(rng):
    d = numbers_of(rng)
    o, e = rng.permutation(N), rng.permutation(8)
    p = rng.integers(0, C, (N, 8, T))
    for i, n in (("x", T), ("k", C)):
        a = d[i].reshape(N, 8, 16, n, 4)
        a[:, :, 0] = 0
        a[:, :, 0, :, 0] = rng.integers(0, 3, (N, 8, n)).astype(np.float32).astype(BF)
        for r in o[2:]:
            a[r, e[0], :8] = 0
            if i == "k": a[r, e[0], 0, :, 0] = 4
            else:
                w = rng.permutation(T)
                go = w // C % 2 == 1
                p[r, e[0]] = w % C
                a[r, e[0], 0, :, 0] = np.where(go, rng.integers(1, 4, T), 0).astype(np.float32).astype(BF)
                a[r, e[0], 1, :, 0] = np.where(go, 0.0, 2.0 ** 24).astype(np.float32).astype(BF)
                p[r, e[1]] = rng.integers(C)
                a[r, e[1], 0, T - 1, 0] = 3
        d[i] = a.reshape(N, 128, 4 * n)
    u = d["u"].reshape(N, 128, 128, 4)
    u[:, :, ::16] = 0
    for r in range(N):
        for h in range(0, 128, 16): u[r, h, h, 0] = 0.0 if r == o[0] else -1.0 if r == o[1] else 1.0
    d["u"] = u.reshape(N, 128, 512)
    return {**d, **pointers(rng), "pt": np.stack([gtable(p[r]) for r in range(N)]), **weights(rng, [0])}
def setup_inputs_near(rng):
    d = numbers_of(rng)
    o = rng.permutation(8)
    sign = np.where(o < 4, 1.0, -1.0)
    for i, n in (("x", T), ("k", C)):
        a = d[i].astype(np.float32).reshape(N, 8, 16, n, 4)
        a[:, :, 0] = 0
        a[:, :, 8:] = 0
        a[:, :, 0, :, 0] = sign[:, None]
        s = rng.integers(0, 16, (N, 8, n))
        a[:, :, 8] = ((s[:, :, :, None] >> np.arange(4)) & 1) * np.exp2(np.arange(4) - 23.0)
        a[:, :, 11, :, 0] = 2.0 ** -10
        for g in range(8):
            if o[g] % 4 == 2:
                a[:, g, 8:] = 0
                a[:, g, 8:10, :, 0] = rng.integers(8, 16, (N, 2, n)) * 2.0 ** -33
            if o[g] == 7:
                a[:, g, 8:] = 0
                a[:, g, 8, :, 0] = 1.96875
                a[:, g, 9, :, 0] = (1.0 + rng.random((N, n))) * np.exp2(-1.0 * rng.integers(13, 17, (N, n)))
            if o[g] % 4 == 1 and i == "x":
                for r in range(N): a[r, g, 0, rng.integers(n), 0] = sign[g] * 2.0 ** 29
        d[i] = a.reshape(N, 128, 4 * n).astype(BF)
    u = d["u"].reshape(N, 128, 128, 4)
    u[:, :, ::16] = 0
    for g in range(8):
        h, c = 16 * g, 1.0 if o[g] % 4 == 0 else 2.0 ** -30
        if o[g] % 4 < 2:
            u[:, h, h, 0] = c
            u[:, h + 11, h, 0] = c
        if o[g] % 4 == 2:
            u[:, h + 8, h, 0] = 1.125 * c
            u[:, h + 9, h, 0] = 1.25 * c if o[g] == 2 else -1.25 * c
        elif o[g] == 7: u[:, h + 9, h, 0] = 1.0
        else: u[:, h + 8, h] = c
    d["u"] = u.reshape(N, 128, 512)
    return {**d, **pointers(rng), **weights(rng, [0, 8, 9, 10, 11, 12, 13, 14, 15])}
def setup_inputs_huge(rng):
    d = numbers_of(rng)
    o = rng.permutation(N)
    for i, n in (("x", T), ("k", C)):
        a = (0.6 + 0.4 * rng.random((N, 128, n, 4))) * 2.0 ** 30
        c = rng.integers(0, 2, (N, 1, n, 1)) * 2.0 - 1.0
        c[o < N // 2] = 1
        d[i] = (a * c).astype(np.float32).reshape(N, 128, 4 * n).astype(BF)
    u = d["u"].reshape(N, 128, 128, 4)
    u[:, :, ::16] = (-2.0 ** 30 * (1 - 0.1 * rng.random((N, 128, 8, 4)))).astype(np.float32).astype(BF)
    d["u"] = u.reshape(N, 128, 512)
    return {**d, **pointers(rng), **weights(rng)}
def setup_inputs_ends(rng):
    d = numbers_of(rng)
    s, h = rng.integers(N), rng.permutation(8)
    o = np.zeros(N, int)
    o[(s - np.arange(N)) % N] = np.concatenate([[0, 2, 1], rng.permutation(np.arange(3, N))])
    e = np.concatenate([rng.permutation((s + np.arange(1, N - 1)) % N)[:2], [s, (s - 1) % N]])
    sign = rng.integers(0, 2, (8, 16, 1, 4)) * 2.0 - 1.0
    sign[h[:2]] = 1
    sign[h[2:4]] = -1
    for r in range(N):
        for i, n in (("x", T), ("k", C)):
            a = np.full((8, 16, n, 4), 2.0 ** -30)
            if o[r] % 2 == 0:
                a = 2.0 ** 30 * (1 - 0.1 * rng.random((8, 16, n, 4)))
                if o[r] == 2:
                    a *= 0.5
                    a[:, :, [0, 1 if i == "x" else C - 1]] = 2.0 ** 30
                a[h[4:6]] = 2.0 ** 30
            if o[r] == 0: a[:] = 2.0 ** 30
            d[i][r] = (a * sign).reshape(128, 4 * n).astype(np.float32).astype(BF)
        c = sign.reshape(128, 4) * (2.0 ** -30 if o[r] % 4 == 1 else 2.0 ** 30) * (-1.0 if o[r] % 4 < 2 else 1.0)
        c = c.astype(np.float32).astype(BF)
        a = d["u"][r].reshape(128, 128, 4).copy()
        a[:, ::16] = c[:, None]
        for g in h[4:6]:
            a[:, 16 * g] = 0
            a[16 * g:16 * g + 16, 16 * g] = c[16 * g:16 * g + 16]
        d["u"][r] = a.reshape(128, 512)
        if o[r] == 0: d["v"][r] = np.tile(c, (1, 128))
    p, a = rng.integers(0, C, (N, 8, T)), rng.integers(0, C, (N, 8, C))
    p[e[0]], a[e[0]] = C - 1, C - 1
    p[e[1]], a[e[1]] = 0, 0
    p[e[2]], a[e[2]] = np.arange(T) % C, np.arange(C)
    p[e[3]], a[e[3]] = (C - 1) * rng.integers(0, 2, (8, T)), C - 1 - np.arange(C)
    p[e[3], :, :4] = [0, C - 1, 0, C - 1]
    d["v"] = (np.where(d["v"] < 0, -1.0, 1.0) * np.where(rng.permutation(N) % 2, 2.0 ** -30, 2.0 ** 30)[:, None, None]).astype(np.float32).astype(BF)
    return {**d, "pt": np.stack([gtable(p[r]) for r in range(N)]), "ad": np.stack([gtable(a[r]) for r in range(N)]), **weights(rng, list(range(16)))}
def setup_inputs_spread(rng):
    d = setup_inputs(rng)
    d["x"] = big(wide(rng, N, 128, 4 * T, cols=6))
    d["k"] = big(wide(rng, N, 128, 4 * C, cols=6))
    return d
def check_inputs(d):
    b = []
    for i in ("x", "k", "u", "v"):
        a = np.abs(d[i].astype(np.float32))
        if not (np.isfinite(a).all() and ((a == 0) | (a >= 2.0 ** -30) & (a <= 2.0 ** 30)).all()): b.append("a value of " + i)
    for i in ("pt", "ad"):
        if not ((d[i] >= 0) & (d[i] < C)).all(): b.append("an entry of " + i)
    none, least, most = [emit(mx_ref.quantize(np.full((128, 16), c, np.float32).astype(BF)))[1][0, 0] for c in (0.0, 2.0 ** -30, 2.0 ** 30)]
    for r in range(N):
        if ((d["wc"][r] & 0x7F) == 0x7F).any(): b.append("wc: a code that is no number")
        s = mx_ref.live(d["ws"][r])
        if ((s != none) & ((s < least) | (s > most))).any(): b.append("ws: a scale out of range")
        a = np.abs(decode(pk(d["wc"][r], d["ws"][r])).astype(np.float64)).reshape(128, 512, 4)
        if not (np.sum(a, axis=(0, 2)) <= 32).all(): b.append("W: the sizes of a column add up to more than 32")
    return b
def half(a, b):
    return ((a.astype(np.float32) + b.astype(np.float32)) * np.float32(0.5)).astype(BF)
def parts(e):
    return np.repeat(np.repeat(e, 16, axis=0), 4, axis=1)
def inserters(s, at, n):
    g = np.arange(8)[:, None]
    o = np.argsort(-s, axis=1, kind="stable")
    place = np.zeros((8, T), np.int64)
    place[g, o] = np.arange(T)
    first = np.full((8, n), T)
    np.minimum.at(first, (np.broadcast_to(g, at.shape), at), place)
    return np.where(first < T, np.take_along_axis(o, np.minimum(first, T - 1), axis=1), -1)
def reference(x, k, u, v, pt, ad, wc, ws):
    qu = [mx_ref.quantize(u[r]) for r in range(N)]
    lay = [pk(wc[r], ws[r]) for r in range(N)]
    now = [x[r] for r in range(N)]
    cell = [decode(mx_ref.quantize(k[r])).astype(BF) for r in range(N)]
    at = [gentries(pt[r]) for r in range(N)]
    near = [gentries(ad[r]) for r in range(N)]
    for n in (C, 2 * C):
        given = []
        slot = []
        for r in range(N):
            q = mx_ref.quantize(now[r])
            own = decode(q).astype(BF)
            win = inserters(mx_ref.matmul(qu[r], q)[::16] + np.float32(0.0), at[r], n)
            a = np.where(parts(win < 0), cell[r], half(cell[r], gcols(own, win)))
            b = np.where(parts(win < 0), cell[r], half(cell[r], gcols(cell[r], near[r])))
            v0, v1 = half(own, gcols(a, at[r])), half(own, gcols(b, at[r]))
            more = mx_ref.matmul(qu[r], mx_ref.quantize(v1))[::16] > mx_ref.matmul(qu[r], mx_ref.quantize(v0))[::16]
            now[r] = np.where(parts(more), v1, v0)
            slot.append(np.where(np.take_along_axis(win, at[r], axis=1) == np.arange(T), at[r], -1))
            given.append(mx_ref.quantize(np.ascontiguousarray(a)))
            at[r] = at[r] + n * more
            near[r] = np.concatenate([np.broadcast_to(np.arange(n) + n, (8, n)), near[r]], axis=1)
            cell[r] = np.concatenate([a, b], axis=1)
        for r in range(N):
            q = given[(r - 1) % N]
            made = tile([mx_ref.matmul(pick(lay[r], np.arange(128 * b, 128 * b + 128)), q) * np.float32(0.03125) for b in range(4)])
            now[r] = np.ascontiguousarray(np.where(parts(slot[r] >= 0), gcols(made, slot[r]), now[r]))
    y, z, op = np.zeros((N, 128, T), np.float32), np.zeros((N, 128, 4 * C), np.float32), np.zeros((N, 8, T), np.float32)
    oc, osc = np.zeros((N, 128, 4 * T), np.uint8), np.zeros((N, 16, T), np.uint8)
    for r in range(N):
        q, qv = mx_ref.quantize(now[r]), mx_ref.quantize(v[r])
        y[r] = mx_ref.matmul(qv, q)
        z[r] = mx_ref.matmul(qv, mx_ref.quantize(np.ascontiguousarray(cell[r])))
        op[r] = at[r]
        oc[r], osc[r] = emit(q)
    return {"y": y, "z": z, "op": op, "oc": oc, "osc": osc}

@@ -1,0 +1,369 @@
+from concourse.mybir import dt, AluOpType, ActivationFunctionType
+
+F32, BF16, I32, U16, F8, U8 = "float32", "bfloat16", "int32", "uint16", "float8_e4m3fn_x4", "uint8"
+NT, NC = 384, 96
+XW = 4 * NT
+GAP = 4096
+WIN = GAP + XW + 4 * 2 * NC
+BIG = 2.0 ** 90
+
+
+def _sb(n, d):
+    return ("sbuf", [128, n], d)
+
+
+SCRATCH = {
+    "xk": _sb(XW + 4 * NC, BF16), "ub": _sb(512, BF16), "vb": _sb(512, BF16), "ptI": _sb(24, I32), "adI": _sb(6, I32),
+    "wq": _sb(512, F8), "wp": _sb(512, U8),
+    "qxk": _sb(NT + NC, F8), "sxk": _sb(NT + NC, U8), "qx2": _sb(NT, F8), "sx2": _sb(NT, U8), "qx3": _sb(NT, F8), "sx3": _sb(NT, U8),
+    "qu": _sb(128, F8), "su": _sb(128, U8), "qur": _sb(128, F8), "sur": _sb(128, U8), "qv": _sb(128, F8), "sv": _sb(128, U8),
+    "qE": _sb(512, F8), "sE": _sb(512, U8),
+    "qa1": _sb(128, F8), "sa1": _sb(128, U8), "qa2": _sb(192, F8), "sa2": _sb(192, U8),
+    "ra1": _sb(128, F8), "rs1": _sb(128, U8), "ra2": _sb(192, F8), "rs2": _sb(192, U8),
+    "q01": _sb(NT, F8), "s01": _sb(NT, U8), "q11": _sb(NT, F8), "s11": _sb(NT, U8),
+    "q02": _sb(NT, F8), "s02": _sb(NT, U8), "q12": _sb(NT, F8), "s12": _sb(NT, U8),
+    "qb": _sb(192, F8), "sb": _sb(192, U8),
+    "half": _sb(128, BF16), "dg": _sb(128, BF16), "ET": _sb(2048, BF16),
+    "pi": _sb(1, I32), "pj": _sb(4, I32), "pf": _sb(4, F32), "IW": _sb(NC, F32), "I4": _sb(NT, BF16), "K16": _sb(12, F32),
+    "c16": _sb(12, F32), "d16": _sb(12, F32), "nb": _sb(12, F32), "uoI": _sb(8, I32), "uo": _sb(8, U16), "IO4": _sb(NT + 2 * NC, F32),
+    "m4": _sb(NT, BF16), "m4s": _sb(NT, BF16), "dp": _sb(NT, BF16), "r4": _sb(NT, BF16),
+    "ad1": _sb(NT + NC, F32), "ad2": _sb(NT + 2 * NC, F32),
+    "pt16": _sb(24, U16), "P1": _sb(NT, BF16), "P2": _sb(NT, BF16), "PM": _sb(NT, BF16), "PS": _sb(NT, BF16),
+    "Lf": _sb(NC, F32), "L41": _sb(NC, U16), "Lt": _sb(NC, F32), "Lg": _sb(NC, F32), "L42": _sb(NC, U16),
+    "pen1": _sb(6 * NT, BF16), "pen2": _sb(12 * NT, BF16), "W": _sb(12 * NT, F32), "MX": _sb(12 * NT, F32), "JK": _sb(12 * NT, BF16),
+    "adf": _sb(12, F32), "cma": _sb(12, F32), "adf2": _sb(12, F32), "cma2": _sb(12, F32),
+    "hh": _sb(24, F32), "ee": _sb(24, F32), "idx": _sb(24, F32), "qf": _sb(24, F32), "tb": _sb(24, F32), "ap": _sb(24, F32),
+    "QL": _sb(160, U16), "BL": _sb(128, U16),
+    "FG1": _sb(XW + 4 * NC, BF16), "FG2": _sb(XW + 8 * NC, BF16), "GC1": _sb(4 * NC, BF16), "GC2": _sb(8 * NC, BF16),
+    "A1": _sb(512, BF16), "B1": _sb(4 * NC, BF16), "AB": _sb(XW, BF16), "AH2": _sb(8 * NC, BF16), "Bg": _sb(XW, BF16),
+    "VW": _sb(WIN, BF16), "X2": _sb(XW, BF16), "X3": _sb(XW, BF16),
+    "Z0": _sb(NT, F32), "Zc": _sb(NT, F32), "CM": _sb(NT, BF16), "CR": _sb(NT, BF16), "CS": _sb(NT, BF16), "SC": _sb(NT, BF16),
+    "AM": _sb(NT, F32), "AS": _sb(NT, F32), "T1": _sb(NC, F32), "EL": _sb(NC, U16), "opr": _sb(NT, F32),
+    "yb": _sb(NT, F32), "zb": _sb(NT, F32),
+}
+for _i in range(8):
+    SCRATCH["p%d" % _i] = ("psum", [128, 512], F32)
+_LOADS = ["pt", "x", "k", "u", "ad", "w", "ws", "v"]
+_STORES = ["op", "y", "z", "oc", "o0", "o1", "o2", "o3"]
+SEMAPHORES = ["cv", "cs", "ct", "cg"] + ["d_" + n for n in _LOADS + _STORES] + ["arr1", "arr2", "sent"]
+
+
+def rank_program(g, core, T, topo):
+    rank = T.rank_of(core)
+    if rank is None:
+        return
+    n_ranks = len(T.cores)
+    nxt = T.cores[(rank + 1) % n_ranks]
+    rid, pid = topo.addr(nxt)[:2]
+    engs = topo.engines(core, nxt)[:8]
+    mask, n_eng = sum(1 << e for e in engs), len(engs)
+    Q = {"v": g.vector, "s": g.scalar, "t": g.tensor, "g": g, "y": g.sync}
+    op_ = AluOpType
+    AF = ActivationFunctionType
+    V, S = g.vector, g.scalar
+
+    count, known, hist, final = {}, {e: {} for e in Q}, {}, {}
+
+    def ap(r):
+        return T[r[0]][:, r[1]:r[2]] if len(r) < 4 or r[3] == 1 else T[r[0]][:, r[1]:r[2]:r[3]]
+
+    def meet(a, b):
+        if a[2] <= b[1] or b[2] <= a[1]:
+            return False
+        sa, sb = (a[3] if len(a) > 3 else 1), (b[3] if len(b) > 3 else 1)
+        return not (sa == sb and sa > 1 and a[1] % sa != b[1] % sa)
+
+    def wait(e, toks):
+        best = {}
+        for t in toks:
+            if t[0] not in best or best[t[0]][1] < t[1]:
+                best[t[0]] = t
+        for t in sorted(best.values(), key=lambda t: -len(t[2])):
+            if known[e].get(t[0], 0) >= t[1]:
+                continue
+            Q[e].wait_ge(T.sem[t[0]], t[1])
+            for k, v in t[2].items():
+                known[e][k] = max(known[e].get(k, 0), v)
+            known[e][t[0]] = max(known[e].get(t[0], 0), t[1])
+
+    def note(r, wr, tok, e):
+        hist.setdefault(r[0], []).append((r, wr, tok, e))
+
+    def do(e, fn, reads, writes, dma=None):
+        toks = []
+        for rs, wr in ((reads, False), (writes, True)):
+            for r in rs:
+                ps = SCRATCH[r[0]][0] == "psum"
+                for (o, ow, tok, oe) in hist.get(r[0], []):
+                    if (wr or ow or (ps and oe != e)) and (ps or meet(r, o)):
+                        toks.append(tok)
+        wait(e, toks)
+        ins = fn()
+        if dma is not None:
+            sem, val = "d_" + dma, 16
+            ins.then_inc(T.sem[sem], 16)
+        else:
+            sem = "c" + e
+            count[sem] = count.get(sem, 0) + 1
+            val = count[sem]
+            ins.then_inc(T.sem[sem], 1)
+        tok = (sem, val, dict(known[e]))
+        final[sem] = tok
+        for r in reads:
+            note(r, False, tok, e)
+        for r in writes:
+            note(r, True, tok, e)
+
+    def load(e, name, dst, src, bc=False):
+        d = ap(dst)
+        if bc:
+            d = d.bitcast(dt.uint8)
+        do(e, lambda: Q[e].dma_start(d, src), [], [dst], dma=name)
+
+    def copy(out, in_):
+        do("v", lambda: V.tensor_copy(ap(out), ap(in_)), [in_], [out])
+
+    def ts(out, in0, s1, s2, o0, o1=None):
+        reads = [in0] + [s for s in (s1, s2) if isinstance(s, tuple)]
+        a = ap(s1) if isinstance(s1, tuple) else s1
+        b = ap(s2) if isinstance(s2, tuple) else s2
+        if o1 is None:
+            do("v", lambda: V.tensor_scalar(ap(out), ap(in0), a, None, o0), reads, [out])
+        else:
+            do("v", lambda: V.tensor_scalar(ap(out), ap(in0), a, b, o0, o1), reads, [out])
+
+    def tt(out, in0, in1, o, off=None):
+        if off is None:
+            do("v", lambda: V.tensor_tensor(ap(out), ap(in0), ap(in1), o), [in0, in1], [out])
+        else:
+            do("v", lambda: V.tensor_tensor(ap(out), ap(in0).indirect(ap(off)), ap(in1), o), [in0, in1, off], [out])
+
+    def scan(out, d0, d1, init, o0, o1):
+        do("v", lambda: V.tensor_tensor_scan(ap(out), ap(d0), ap(d1), init, o0, o1), [d0, d1], [out])
+
+    def act(out, in_, func=AF.Copy, scale=1.0, bias=None, acc=None, off=None):
+        reads, writes = [in_], [out]
+        kw = {}
+        if bias is not None:
+            reads.append(bias)
+            kw["bias"] = ap(bias)
+        if scale != 1.0:
+            kw["scale"] = scale
+        if acc is not None:
+            writes.append(acc)
+            kw["accum_out"] = ap(acc)
+        src = ap(in_)
+        if off is not None:
+            reads.append(off)
+            src = src.indirect(ap(off))
+        do("s", lambda: S.activation(ap(out), src, func, **kw), reads, writes)
+
+    def quant(qb, sb, a, b, src):
+        do("v", lambda: V.quantize_mx(T[qb][:, a:b], T[sb][:, a:b], ap(src)), [src], [(qb, a, b), (sb, a, b)])
+
+    def mm(bank, lq, ls, la, rq, rs, ra, rb):
+        do("t", lambda: g.tensor.matmul_mx(T[bank][:, 0:rb - ra], T[lq][:, la:la + 128], T[ls][:, la:la + 128],
+                                           T[rq][:, ra:rb], T[rs][:, ra:rb], True, True),
+           [(lq, la, la + 128), (ls, la, la + 128), (rq, ra, rb), (rs, ra, rb)], [(bank, 0, 512)])
+
+    def bank(i, n):
+        return ("p%d" % i, 0, n)
+
+    def iota(out, pattern, base=0, cm=0):
+        imp = SCRATCH[out[0]][2] != I32
+        if imp:
+            do("g", lambda: g.iota(ap(out), pattern, base, cm, allow_small_or_imprecise_dtypes=True), [], [out])
+        else:
+            do("g", lambda: g.iota(ap(out), pattern, base, cm), [], [out])
+
+    def fill(out, c):
+        do("v", lambda: V.memset(ap(out), c), [], [out])
+
+    load("y", "pt", ("ptI", 0, 24), T.pt[:])
+    load("s", "u", ("ub", 0, 512), T.u[:])
+    load("y", "x", ("xk", 0, XW), T.x[:])
+    load("s", "k", ("xk", XW, XW + 4 * NC), T.k[:])
+    load("y", "ad", ("adI", 0, 6), T.ad[:])
+    load("y", "w", ("wq", 0, 512), T.wc[:], bc=True)
+    load("y", "ws", ("wp", 0, 512), T.ws[:])
+    load("y", "v", ("vb", 0, 512), T.v[:])
+
+    fill(("half", 0, 128), 0.5)
+    iota(("pi", 0, 1), [[0, 1]], 0, 1)
+    iota(("IW", 0, NC), [[1, NC]])
+    iota(("K16", 0, 12), [[16, 12]])
+    do("g", lambda: g.affine_select(T.dg[:], T.half[:], [[-1, 128]], op_.is_equal, 0.0, 0, 1), [("half", 0, 128)], [("dg", 0, 128)])
+    iota(("uoI", 0, 8), [[16, 8]])
+    iota(("I4", 0, NT), [[0, NT // 4], [1, 4]])
+    fill(("ET", 0, 2048), 0.0)
+    for b in range(4):
+        act(("ET", 512 * b + b, 512 * b + 512, 4), ("dg", 0, 128))
+    iota(("IO4", 0, NT + 2 * NC), [[4, NT + 2 * NC]])
+    iota(("ad1", 0, NT), [[4, NT]])
+    iota(("VW", XW + 4 * NC, GAP), [[0, GAP - XW - 4 * NC]])
+    iota(("VW", GAP + XW + 4 * NC, WIN), [[0, 4 * NC]])
+    iota(("ad2", 0, NT), [[4, NT]])
+    ts(("pj", 0, 1), ("pi", 0, 1), 15, None, op_.bitwise_and)
+    ts(("pj", 1, 2), ("pi", 0, 1), 15, 2, op_.bitwise_and, op_.logical_shift_right)
+    ts(("pj", 2, 3), ("pi", 0, 1), 3, None, op_.bitwise_and)
+    copy(("pf", 0, 3), ("pj", 0, 3))
+    QP, RP, TP = ("pf", 0, 1), ("pf", 1, 2), ("pf", 2, 3)
+    ts(("c16", 0, 12), ("K16", 0, 12), QP, None, op_.add)
+    ts(("nb", 0, 12), ("c16", 0, 12), -BIG, None, op_.mult)
+    ts(("d16", 0, 12), ("c16", 0, 12), float(NT), None, op_.add)
+    copy(("uo", 0, 8), ("uoI", 0, 8))
+    quant("qE", "sE", 0, 512, ("ET", 0, 2048))
+    ts(("m4", 0, NT), ("I4", 0, NT), RP, None, op_.is_equal)
+    ts(("m4s", 0, NT), ("I4", 0, NT), RP, 1.0 / GAP, op_.is_equal, op_.mult)
+    ts(("dp", 0, NT), ("I4", 0, NT), RP, BIG, op_.not_equal, op_.mult)
+    ts(("r4", 0, NT), ("I4", 0, NT), 0.0, None, op_.not_equal)
+    fill(("A1", 4 * NC, 512), 0.0)
+
+    def pen_v(pen, row, k):
+        ts((pen, k * NT, (k + 1) * NT), (row, 0, NT), ("c16", k, k + 1), BIG, op_.not_equal, op_.mult)
+
+    def pen_s(pen, row, k):
+        act((pen, k * NT, (k + 1) * NT), (row, 0, NT), AF.Abs, BIG, ("nb", k, k + 1))
+
+    copy(("pt16", 0, 24), ("ptI", 0, 24))
+    do("v", lambda: V.tensor_copy(T.P1[:, 0:NT], T.IW[:, 0:NC].indirect(T.pt16[:, 0:24])), [("IW", 0, NC), ("pt16", 0, 24)], [("P1", 0, NT)])
+    for k in (3, 4):
+        pen_s("pen1", "P1", k)
+    quant("qu", "su", 0, 128, ("ub", 0, 512))
+    do("v", lambda: V.tensor_copy(T.qur[:, 0:128].bitcast(dt.uint32), T.qu[:, 0:128].bitcast(dt.uint32).indirect(T.uo[:, 0:8])),
+       [("qu", 0, 128), ("uo", 0, 8)], [("qur", 0, 128)])
+    act(("sur", 0, 128), ("su", 0, 128), off=("uo", 0, 8))
+    pen_s("pen1", "P1", 5)
+    for k in (0, 1):
+        pen_v("pen1", "P1", k)
+    quant("qxk", "sxk", 0, NT + NC, ("xk", 0, XW + 4 * NC))
+    mm("p4", "qur", "sur", 0, "qxk", "sxk", 0, NT)
+    for b in range(4):
+        mm("p%d" % b, "qE", "sE", 128 * b, "qxk", "sxk", 0, NT + NC)
+    pen_v("pen1", "P1", 2)
+    tt(("PM", 0, NT), ("P1", 0, NT), ("m4", 0, NT), op_.mult)
+    scan(("PS", 0, NT), ("r4", 0, NT), ("PM", 0, NT), 0.0, op_.mult, op_.add)
+    ts(("Lf", 0, NC), ("PS", 3, NT, 4), 4.0, TP, op_.mult, op_.add)
+    ts(("L41", 0, NC), ("PS", 3, NT, 4), 4.0, TP, op_.mult, op_.add)
+    copy(("adf", 0, 6), ("adI", 0, 6))
+    tt(("cma", 0, 6), ("c16", 0, 6), ("adf", 0, 6), op_.subtract)
+    copy(("adf2", 0, 6), ("c16", 6, 12))
+    copy(("adf2", 6, 12), ("adf", 0, 6))
+    tt(("cma2", 0, 12), ("c16", 0, 12), ("adf2", 0, 12), op_.subtract)
+
+    for rnd in (0, 1):
+        M = NC << rnd
+        K = M // 16
+        pen, adf, cma = ("pen1", "adf", "cma") if rnd == 0 else ("pen2", "adf2", "cma2")
+        FG, GC, A = ("FG1", "GC1", "A1") if rnd == 0 else ("FG2", "GC2", "AB")
+        L4 = ("L41" if rnd == 0 else "L42", 0, NC)
+        AD = "ad1" if rnd == 0 else "ad2"
+        h0 = 12 * rnd
+        fb = list(range(4))
+        for k in range(K):
+            w = ("W", k * NT, (k + 1) * NT)
+            if rnd == 1 and k < 7:
+                pen_v(pen, "P2", k)
+            tt(w, bank(4, NT), (pen, k * NT, (k + 1) * NT), op_.subtract)
+            scan(("MX", k * NT, (k + 1) * NT), w, w, -2.0 ** 80, op_.max, op_.max)
+            act(("JK", k * NT, (k + 1) * NT), ("MX", k * NT, (k + 1) * NT), AF.Sign, -1.0, ("MX", k * NT + NT - 1, k * NT + NT), ("idx", h0 + k, h0 + k + 1))
+            if fb and k >= 1 + 2 * rnd:
+                b = fb.pop(0)
+                n = NT + NC if rnd == 0 else NT
+                act((FG, b, 4 * n, 4), bank(b, n))
+                if not fb and rnd == 0:
+                    act(("GC1", 0, 4 * NC), ("FG1", XW, XW + 4 * NC))
+        H, E = ("hh", h0, h0 + K), ("ee", h0, h0 + K)
+        ts(H, ("MX", NT - 1, K * NT, NT), -2.0 ** 75, None, op_.is_le)
+        tt(("tb", h0, h0 + K), H, (cma, 0, K), op_.mult)
+        tt(("ap", h0, h0 + K), ("tb", h0, h0 + K), (adf, 0, K), op_.add)
+        for t in range(4):
+            ts(("BL", 64 * rnd + 16 * t, 64 * rnd + 16 * t + K), ("ap", h0, h0 + K), 4.0, float(t), op_.mult, op_.add)
+        tt(E, H, ("d16", 0, K), op_.mult)
+        AH, B = (("FG2", XW, XW + 4 * M), ("B1", 0, 4 * M)) if rnd == 0 else (("AH2", 0, 4 * M), ("AB", 4 * M, 8 * M))
+        for t in range(4):
+            tt((B[0], B[1] + t, B[2], 4), (FG, XW, XW + 4 * M), (GC, t, 4 * M, 4), op_.add, ("BL", 64 * rnd + 16 * t, 64 * rnd + 16 * t + K))
+        act(("Bg", 0, XW), B, scale=0.5, off=L4)
+        QF = ("qf", h0, h0 + K)
+        tt(QF, ("idx", h0, h0 + K), E, op_.add)
+        for t in range(4):
+            ts(("QL", 80 * rnd + 16 * t, 80 * rnd + 16 * t + K), QF, 4.0, float(t), op_.mult, op_.add)
+        for t in range(4):
+            tt((A, t, 4 * M, 4), (FG, 0, XW + 4 * M), (GC, t, 4 * M, 4), op_.add, ("QL", 80 * rnd + 16 * t, 80 * rnd + 16 * t + K))
+        qa, sa, ra, rs = ("qa1", "sa1", "ra1", "rs1") if rnd == 0 else ("qa2", "sa2", "ra2", "rs2")
+        nA = max(M, 128)
+        quant(qa, sa, 0, nA, (A, 0, 4 * nA))
+        wait("g", [hist[qa][-1][2]])
+        arr = T.sem["arr%d" % (rnd + 1)]
+        g.remote_dma(T[ra][:, 0:nA].bitcast(dt.uint8), T[qa][:, 0:nA].bitcast(dt.uint8), arr, T.sem.sent, pid, rid, mask)
+        g.remote_dma(T[rs][:, 0:nA], T[sa][:, 0:nA], arr, T.sem.sent, pid, rid, mask)
+        atok = ("arr%d" % (rnd + 1), 2 * n_eng, {})
+        note((ra, 0, nA), True, atok, "g")
+        note((rs, 0, nA), True, atok, "g")
+        final["arr%d" % (rnd + 1)] = atok
+        ts(AH, (A, 0, 4 * M), 0.5, None, op_.mult)
+        q0, s0, q1, s1 = ["%s%d" % (c, rnd + 1) for c in ("q0", "s0", "q1", "s1")]
+        tt(("VW", 0, XW), AH, (FG, 0, XW), op_.add, L4)
+        quant(q0, s0, 0, NT, ("VW", 0, XW))
+        mm("p5", "qur", "sur", 0, q0, s0, 0, NT)
+        copy(("QL", 80 * rnd + 64, 80 * rnd + 64 + K), QF)
+        do("v", lambda: V.tensor_copy(T[AD][:, 0:NT + M].indirect(T.QL[:, 80 * rnd + 64:80 * rnd + 64 + K]), T.IO4[:, NT:NT + M]),
+           [("IO4", NT, NT + M), ("QL", 80 * rnd + 64, 80 * rnd + 64 + K)], [(AD, 0, NT + M)])
+        for b in range(4):
+            tt(("VW", GAP + b, GAP + XW, 4), bank(b, NT), ("Bg", b, XW, 4), op_.add)
+        quant(q1, s1, 0, NT, ("VW", GAP, GAP + XW))
+        for b in range(4):
+            pb = 7 if b % 2 == 0 else 4
+            mm("p%d" % pb, "wq", "wp", 128 * b, ra, rs, 0, nA)
+            act(("VW", XW + b, XW + 4 * M, 4), bank(pb, M), scale=0.03125)
+        act(("VW", GAP + XW, GAP + XW + 4 * M), ("VW", XW, XW + 4 * M))
+        mm("p6", "qur", "sur", 0, q1, s1, 0, NT)
+        tt(("Z0", 0, NT), bank(5, NT), ("dp", 0, NT), op_.add)
+        act(("Zc", 0, NT), bank(5, NT))
+        tt(("AM", 0, NT), (AD, 0, NT), ("m4s", 0, NT), op_.mult)
+        scan(("AS", 0, NT), ("r4", 0, NT), ("AM", 0, NT), 0.0, op_.mult, op_.add)
+        if rnd == 1:
+            quant("qv", "sv", 0, 128, ("vb", 0, 512))
+            quant("qb", "sb", 0, M, B)
+            mm("p0", "qv", "sv", 0, qa, sa, 0, M)
+            mm("p1", "qv", "sv", 0, "qb", "sb", 0, M)
+        tt(("CM", 0, NT), bank(6, NT), ("Z0", 0, NT), op_.is_gt)
+        scan(("SC", 0, NT), ("r4", 0, NT), ("CM", 0, NT), 0.0, op_.mult, op_.add)
+        tt(("T1", 0, NC), ("SC", 3, NT, 4), ("AS", 3, NT, 4), op_.add)
+        ts(("EL", 0, NC), ("T1", 0, NC), float(GAP), TP, op_.mult, op_.add)
+        X, qx, sx = ("X2", "qx2", "sx2") if rnd == 0 else ("X3", "qx3", "sx3")
+        cut = 44
+        act((X, 16 * cut, XW), ("VW", 0, WIN), off=("EL", cut, NC))
+        do("v", lambda: V.tensor_copy(T[X][:, 0:16 * cut], T.VW[:, 0:WIN].indirect(T.EL[:, 0:cut])), [("VW", 0, WIN), ("EL", 0, cut)], [(X, 0, 16 * cut)])
+        quant(qx, sx, 0, 4 * cut, (X, 0, 16 * cut))
+        quant(qx, sx, 4 * cut, NT, (X, 16 * cut, XW))
+        if rnd == 0:
+            mm("p4", "qur", "sur", 0, qx, sx, 0, NT)
+            for b in range(4):
+                mm("p%d" % b, "qE", "sE", 128 * b, qx, sx, 0, NT)
+            tt(("CR", 0, NT), bank(6, NT), ("Zc", 0, NT), op_.is_gt)
+            ts(("CS", 0, NT), ("CR", 0, NT), float(M), None, op_.mult)
+            tt(("P2", 0, NT), ("P1", 0, NT), ("CS", 0, NT), op_.add)
+            for k in range(7, 12):
+                pen_s("pen2", "P2", k)
+            act(("FG2", XW + 4 * NC, XW + 8 * NC), ("B1", 0, 4 * NC), scale=0.5)
+            act(("GC2", 0, 8 * NC), ("FG2", XW, XW + 8 * NC))
+            ts(("Lt", 0, NC), ("SC", 3, NT, 4), 4.0 * M, None, op_.mult)
+            tt(("Lg", 0, NC), ("Lt", 0, NC), ("Lf", 0, NC), op_.add)
+            copy(("L42", 0, NC), ("Lg", 0, NC))
+        else:
+            act(("zb", 0, M), bank(0, M))
+            act(("zb", M, 2 * M), bank(1, M))
+            do("y", lambda: g.sync.dma_start(T.z[:], T.zb[:]), [("zb", 0, NT)], [], dma="z")
+            mm("p7", "qv", "sv", 0, qx, sx, 0, NT)
+            act(("yb", 0, NT), bank(7, NT))
+            do("s", lambda: S.dma_start(T.y[:], T.yb[:]), [("yb", 0, NT)], [], dma="y")
+            do("y", lambda: g.sync.dma_start(T.oc[:], T.qx3[:, 0:NT].bitcast(dt.uint8)), [("qx3", 0, NT)], [], dma="oc")
+            for i in range(4):
+                do("y", lambda: g.sync.dma_start(T.osc[4 * i:4 * i + 4, 0:NT], T.sx3[32 * i:32 * i + 4, 0:NT]), [("sx3", 0, NT)], [], dma="o%d" % i)
+            tt(("CR", 0, NT), bank(6, NT), ("Zc", 0, NT), op_.is_gt)
+            ts(("CS", 0, NT), ("CR", 0, NT), float(M), None, op_.mult)
+            tt(("opr", 0, NT), ("P2", 0, NT), ("CS", 0, NT), op_.add)
+            do("y", lambda: g.sync.dma_start(T.op[:], T.opr[0:128:16, 0:NT]), [("opr", 0, NT)], [], dma="op")
+    g.wait_ge(T.sem.sent, 4 * n_eng)
+    wait("y", list(final.values()))

@@ -6,6 +6,9 @@ XW = 4 * NT
 GAP = 4096
 WIN = GAP + XW + 4 * 2 * NC
 BIG = 2.0 ** 90
+CUT = (20, 36)
+PEN_S = (2, 3)
+BC = (24, 0)
 
 
 def _sb(n, d):
@@ -14,52 +17,43 @@ def _sb(n, d):
 
 SCRATCH = {
     "xk": _sb(XW + 4 * NC, BF16), "ub": _sb(512, BF16), "vb": _sb(512, BF16), "ptI": _sb(24, I32), "adI": _sb(6, I32),
-    "wq": _sb(512, F8), "wp": _sb(512, U8),
-    "qxk": _sb(NT + NC, F8), "sxk": _sb(NT + NC, U8), "qx2": _sb(NT, F8), "sx2": _sb(NT, U8), "qx3": _sb(NT, F8), "sx3": _sb(NT, U8),
-    "qu": _sb(128, F8), "su": _sb(128, U8), "qur": _sb(128, F8), "sur": _sb(128, U8), "qv": _sb(128, F8), "sv": _sb(128, U8),
-    "qE": _sb(512, F8), "sE": _sb(512, U8),
-    "qa1": _sb(128, F8), "sa1": _sb(128, U8), "qa2": _sb(192, F8), "sa2": _sb(192, U8),
-    "ra1": _sb(128, F8), "rs1": _sb(128, U8), "ra2": _sb(192, F8), "rs2": _sb(192, U8),
-    "q01": _sb(NT, F8), "s01": _sb(NT, U8), "q11": _sb(NT, F8), "s11": _sb(NT, U8),
-    "q02": _sb(NT, F8), "s02": _sb(NT, U8), "q12": _sb(NT, F8), "s12": _sb(NT, U8),
-    "qb": _sb(192, F8), "sb": _sb(192, U8),
     "half": _sb(128, BF16), "dg": _sb(128, BF16), "ET": _sb(2048, BF16),
-    "pi": _sb(1, I32), "pj": _sb(4, I32), "pf": _sb(4, F32), "IW": _sb(NC, F32), "I4": _sb(NT, BF16), "K16": _sb(12, F32),
+    "pi": _sb(1, I32), "pj": _sb(4, I32), "pf": _sb(4, F32), "IW": _sb(NC, F32), "R4": _sb(4, F32), "K16": _sb(12, F32), "I4": _sb(NT, BF16),
+    "cm": _sb(4, F32), "cs": _sb(4, F32), "cn": _sb(4, F32), "r4": _sb(NT, BF16),
     "c16": _sb(12, F32), "d16": _sb(12, F32), "nb": _sb(12, F32), "uoI": _sb(8, I32), "uo": _sb(8, U16), "IO4": _sb(NT + 2 * NC, F32),
-    "m4": _sb(NT, BF16), "m4s": _sb(NT, BF16), "dp": _sb(NT, BF16), "r4": _sb(NT, BF16),
     "ad1": _sb(NT + NC, F32), "ad2": _sb(NT + 2 * NC, F32),
     "pt16": _sb(24, U16), "P1": _sb(NT, BF16), "P2": _sb(NT, BF16), "PM": _sb(NT, BF16), "PS": _sb(NT, BF16),
     "Lf": _sb(NC, F32), "L41": _sb(NC, U16), "Lt": _sb(NC, F32), "Lg": _sb(NC, F32), "L42": _sb(NC, U16),
     "pen1": _sb(6 * NT, BF16), "pen2": _sb(12 * NT, BF16), "W": _sb(12 * NT, F32), "MX": _sb(12 * NT, F32), "JK": _sb(12 * NT, BF16),
-    "adf": _sb(12, F32), "cma": _sb(12, F32), "adf2": _sb(12, F32), "cma2": _sb(12, F32),
-    "hh": _sb(24, F32), "ee": _sb(24, F32), "idx": _sb(24, F32), "qf": _sb(24, F32), "tb": _sb(24, F32), "ap": _sb(24, F32),
-    "QL": _sb(160, U16), "BL": _sb(128, U16),
-    "FG1": _sb(XW + 4 * NC, BF16), "FG2": _sb(XW + 8 * NC, BF16), "GC1": _sb(4 * NC, BF16), "GC2": _sb(8 * NC, BF16),
-    "A1": _sb(512, BF16), "B1": _sb(4 * NC, BF16), "AB": _sb(XW, BF16), "AH2": _sb(8 * NC, BF16), "Bg": _sb(XW, BF16),
+    "cma": _sb(12, F32), "cma2": _sb(12, F32), "hh": _sb(24, F32),
+    "ix1": _sb(12, F32), "ix2": _sb(24, F32), "ea1": _sb(12, F32), "ea2": _sb(24, F32), "qp1": _sb(12, F32), "qp2": _sb(24, F32),
+    "QB1": _sb(12, U16), "QB2": _sb(24, U16),
+    "FG1": _sb(4 * (NT + NC), BF16), "FG2": _sb(4 * (NT + 2 * NC), BF16), "GC1": _sb(4 * NC, BF16), "GC2": _sb(8 * NC, BF16),
+    "A1": _sb(512, BF16), "B1": _sb(4 * NC, BF16), "AB": _sb(XW, BF16), "Ag": _sb(XW, BF16), "Bg": _sb(XW, BF16),
     "VW": _sb(WIN, BF16), "X2": _sb(XW, BF16), "X3": _sb(XW, BF16),
-    "Z0": _sb(NT, F32), "Zc": _sb(NT, F32), "CM": _sb(NT, BF16), "CR": _sb(NT, BF16), "CS": _sb(NT, BF16), "SC": _sb(NT, BF16),
-    "AM": _sb(NT, F32), "AS": _sb(NT, F32), "T1": _sb(NC, F32), "EL": _sb(NC, U16), "opr": _sb(NT, F32),
+    "Z0": _sb(NT, F32), "Zc": _sb(NT, F32), "CM": _sb(NT, BF16), "CR": _sb(NT, BF16), "CS": _sb(NT, BF16), "SC": _sb(NT + 4, F32),
+    "AM": _sb(NT, F32), "T1": _sb(NC, F32), "EL": _sb(NC, U16), "opr": _sb(NT, F32),
     "yb": _sb(NT, F32), "zb": _sb(NT, F32),
 }
+for _n, _w in (("w", 512), ("xk", NT + NC), ("x2", NT), ("x3", NT), ("u", 128), ("ur", 128), ("v", 128), ("E", 512), ("a1", 128), ("a2", 192),
+               ("r1", 128), ("r2", 192), ("01", NT), ("11", NT), ("02", NT), ("12", NT), ("b", 192)):
+    SCRATCH["q" + _n], SCRATCH["s" + _n] = _sb(_w, F8), _sb(_w, U8)
 for _i in range(8):
     SCRATCH["p%d" % _i] = ("psum", [128, 512], F32)
-_LOADS = ["pt", "x", "k", "u", "ad", "w", "ws", "v"]
-_STORES = ["op", "y", "z", "oc", "o0", "o1", "o2", "o3"]
-SEMAPHORES = ["cv", "cs", "ct", "cg"] + ["d_" + n for n in _LOADS + _STORES] + ["arr1", "arr2", "sent"]
+_DMAS = ["pt", "x", "k", "u", "ad", "w", "ws", "v", "op", "y0", "y1", "z", "oc", "o0", "o1", "o2", "o3"]
+SEMAPHORES = ["cv", "cs", "ct", "cg"] + ["d_" + n for n in _DMAS] + ["arr1", "arr2", "sent"]
 
 
 def rank_program(g, core, T, topo):
     rank = T.rank_of(core)
     if rank is None:
         return
-    n_ranks = len(T.cores)
-    nxt = T.cores[(rank + 1) % n_ranks]
+    nxt = T.cores[(rank + 1) % len(T.cores)]
     rid, pid = topo.addr(nxt)[:2]
     engs = topo.engines(core, nxt)[:8]
     mask, n_eng = sum(1 << e for e in engs), len(engs)
     Q = {"v": g.vector, "s": g.scalar, "t": g.tensor, "g": g, "y": g.sync}
-    op_ = AluOpType
-    AF = ActivationFunctionType
+    op_, AF = AluOpType, ActivationFunctionType
     V, S = g.vector, g.scalar
 
     count, known, hist, final = {}, {e: {} for e in Q}, {}, {}
@@ -99,15 +93,10 @@ def rank_program(g, core, T, topo):
                         toks.append(tok)
         wait(e, toks)
         ins = fn()
-        if dma is not None:
-            sem, val = "d_" + dma, 16
-            ins.then_inc(T.sem[sem], 16)
-        else:
-            sem = "c" + e
-            count[sem] = count.get(sem, 0) + 1
-            val = count[sem]
-            ins.then_inc(T.sem[sem], 1)
-        tok = (sem, val, dict(known[e]))
+        sem, n = ("d_" + dma, 16) if dma is not None else ("c" + e, 1)
+        count[sem] = count.get(sem, 0) + n
+        ins.then_inc(T.sem[sem], n)
+        tok = (sem, count[sem], dict(known[e]))
         final[sem] = tok
         for r in reads:
             note(r, False, tok, e)
@@ -115,66 +104,69 @@ def rank_program(g, core, T, topo):
             note(r, True, tok, e)
 
     def load(e, name, dst, src, bc=False):
-        d = ap(dst)
-        if bc:
-            d = d.bitcast(dt.uint8)
+        d = ap(dst).bitcast(dt.uint8) if bc else ap(dst)
         do(e, lambda: Q[e].dma_start(d, src), [], [dst], dma=name)
+
+    def store(e, name, dst, src, rd):
+        do(e, lambda: Q[e].dma_start(dst, src), [rd], [], dma=name)
 
     def copy(out, in_):
         do("v", lambda: V.tensor_copy(ap(out), ap(in_)), [in_], [out])
 
-    def ts(out, in0, s1, s2, o0, o1=None):
-        reads = [in0] + [s for s in (s1, s2) if isinstance(s, tuple)]
+    def ts(out, in0, s1, s2, o0, o1=None, off=None):
+        reads = [in0] + [s for s in (s1, s2, off) if isinstance(s, tuple)]
         a = ap(s1) if isinstance(s1, tuple) else s1
         b = ap(s2) if isinstance(s2, tuple) else s2
+        src = ap(in0) if off is None else ap(in0).indirect(ap(off))
         if o1 is None:
-            do("v", lambda: V.tensor_scalar(ap(out), ap(in0), a, None, o0), reads, [out])
+            do("v", lambda: V.tensor_scalar(ap(out), src, a, None, o0), reads, [out])
         else:
-            do("v", lambda: V.tensor_scalar(ap(out), ap(in0), a, b, o0, o1), reads, [out])
+            do("v", lambda: V.tensor_scalar(ap(out), src, a, b, o0, o1), reads, [out])
 
     def tt(out, in0, in1, o, off=None):
-        if off is None:
-            do("v", lambda: V.tensor_tensor(ap(out), ap(in0), ap(in1), o), [in0, in1], [out])
-        else:
-            do("v", lambda: V.tensor_tensor(ap(out), ap(in0).indirect(ap(off)), ap(in1), o), [in0, in1, off], [out])
+        src = ap(in0) if off is None else ap(in0).indirect(ap(off))
+        do("v", lambda: V.tensor_tensor(ap(out), src, ap(in1), o), [in0, in1] + ([] if off is None else [off]), [out])
+
+    def pick(out, in_, off):
+        do("v", lambda: V.tensor_copy(ap(out), ap(in_).indirect(ap(off))), [in_, off], [out])
+
+    def put(out, in_, off):
+        do("v", lambda: V.tensor_copy(ap(out).indirect(ap(off)), ap(in_)), [in_, off], [out])
 
     def scan(out, d0, d1, init, o0, o1):
         do("v", lambda: V.tensor_tensor_scan(ap(out), ap(d0), ap(d1), init, o0, o1), [d0, d1], [out])
 
     def act(out, in_, func=AF.Copy, scale=1.0, bias=None, acc=None, off=None):
-        reads, writes = [in_], [out]
-        kw = {}
+        reads, writes, kw, src = [in_], [out], {}, ap(in_)
         if bias is not None:
             reads.append(bias)
             kw["bias"] = ap(bias)
-        if scale != 1.0:
+        if isinstance(scale, tuple):
+            reads.append(scale)
+            kw["scale"] = ap(scale)
+        elif scale != 1.0:
             kw["scale"] = scale
         if acc is not None:
             writes.append(acc)
             kw["accum_out"] = ap(acc)
-        src = ap(in_)
         if off is not None:
             reads.append(off)
             src = src.indirect(ap(off))
         do("s", lambda: S.activation(ap(out), src, func, **kw), reads, writes)
 
-    def quant(qb, sb, a, b, src):
-        do("v", lambda: V.quantize_mx(T[qb][:, a:b], T[sb][:, a:b], ap(src)), [src], [(qb, a, b), (sb, a, b)])
+    def quant(n, a, b, src):
+        do("v", lambda: V.quantize_mx(T["q" + n][:, a:b], T["s" + n][:, a:b], ap(src)), [src], [("q" + n, a, b), ("s" + n, a, b)])
 
-    def mm(bank, lq, ls, la, rq, rs, ra, rb):
-        do("t", lambda: g.tensor.matmul_mx(T[bank][:, 0:rb - ra], T[lq][:, la:la + 128], T[ls][:, la:la + 128],
-                                           T[rq][:, ra:rb], T[rs][:, ra:rb], True, True),
-           [(lq, la, la + 128), (ls, la, la + 128), (rq, ra, rb), (rs, ra, rb)], [(bank, 0, 512)])
+    def mm(pb, ln, la, rn, ra, rb):
+        lq, ls, rq, rs = ("q" + ln, la, la + 128), ("s" + ln, la, la + 128), ("q" + rn, ra, rb), ("s" + rn, ra, rb)
+        do("t", lambda: g.tensor.matmul_mx(T["p%d" % pb][:, 0:rb - ra], ap(lq), ap(ls), ap(rq), ap(rs), True, True), [lq, ls, rq, rs], [("p%d" % pb, 0, 512)])
 
-    def bank(i, n):
-        return ("p%d" % i, 0, n)
+    def bank(i, n, a=0, st=1):
+        return ("p%d" % i, a, n, st)
 
     def iota(out, pattern, base=0, cm=0):
-        imp = SCRATCH[out[0]][2] != I32
-        if imp:
-            do("g", lambda: g.iota(ap(out), pattern, base, cm, allow_small_or_imprecise_dtypes=True), [], [out])
-        else:
-            do("g", lambda: g.iota(ap(out), pattern, base, cm), [], [out])
+        kw = {} if SCRATCH[out[0]][2] == I32 else {"allow_small_or_imprecise_dtypes": True}
+        do("g", lambda: g.iota(ap(out), pattern, base, cm, **kw), [], [out])
 
     def fill(out, c):
         do("v", lambda: V.memset(ap(out), c), [], [out])
@@ -184,14 +176,15 @@ def rank_program(g, core, T, topo):
     load("y", "x", ("xk", 0, XW), T.x[:])
     load("s", "k", ("xk", XW, XW + 4 * NC), T.k[:])
     load("y", "ad", ("adI", 0, 6), T.ad[:])
-    load("y", "w", ("wq", 0, 512), T.wc[:], bc=True)
-    load("y", "ws", ("wp", 0, 512), T.ws[:])
+    load("y", "w", ("qw", 0, 512), T.wc[:], bc=True)
+    load("y", "ws", ("sw", 0, 512), T.ws[:])
     load("y", "v", ("vb", 0, 512), T.v[:])
 
     fill(("half", 0, 128), 0.5)
     iota(("pi", 0, 1), [[0, 1]], 0, 1)
     iota(("IW", 0, NC), [[1, NC]])
     iota(("K16", 0, 12), [[16, 12]])
+    iota(("R4", 0, 4), [[1, 4]])
     do("g", lambda: g.affine_select(T.dg[:], T.half[:], [[-1, 128]], op_.is_equal, 0.0, 0, 1), [("half", 0, 128)], [("dg", 0, 128)])
     iota(("uoI", 0, 8), [[16, 8]])
     iota(("I4", 0, NT), [[0, NT // 4], [1, 4]])
@@ -209,15 +202,12 @@ def rank_program(g, core, T, topo):
     copy(("pf", 0, 3), ("pj", 0, 3))
     QP, RP, TP = ("pf", 0, 1), ("pf", 1, 2), ("pf", 2, 3)
     ts(("c16", 0, 12), ("K16", 0, 12), QP, None, op_.add)
+    ts(("cm", 0, 4), ("R4", 0, 4), RP, None, op_.is_equal)
     ts(("nb", 0, 12), ("c16", 0, 12), -BIG, None, op_.mult)
-    ts(("d16", 0, 12), ("c16", 0, 12), float(NT), None, op_.add)
     copy(("uo", 0, 8), ("uoI", 0, 8))
-    quant("qE", "sE", 0, 512, ("ET", 0, 2048))
-    ts(("m4", 0, NT), ("I4", 0, NT), RP, None, op_.is_equal)
-    ts(("m4s", 0, NT), ("I4", 0, NT), RP, 1.0 / GAP, op_.is_equal, op_.mult)
-    ts(("dp", 0, NT), ("I4", 0, NT), RP, BIG, op_.not_equal, op_.mult)
-    ts(("r4", 0, NT), ("I4", 0, NT), 0.0, None, op_.not_equal)
-    fill(("A1", 4 * NC, 512), 0.0)
+    copy(("pt16", 0, 24), ("ptI", 0, 24))
+    quant("E", 0, 512, ("ET", 0, 2048))
+    pick(("P1", 0, NT), ("IW", 0, NC), ("pt16", 0, 24))
 
     def pen_v(pen, row, k):
         ts((pen, k * NT, (k + 1) * NT), (row, 0, NT), ("c16", k, k + 1), BIG, op_.not_equal, op_.mult)
@@ -225,145 +215,168 @@ def rank_program(g, core, T, topo):
     def pen_s(pen, row, k):
         act((pen, k * NT, (k + 1) * NT), (row, 0, NT), AF.Abs, BIG, ("nb", k, k + 1))
 
-    copy(("pt16", 0, 24), ("ptI", 0, 24))
-    do("v", lambda: V.tensor_copy(T.P1[:, 0:NT], T.IW[:, 0:NC].indirect(T.pt16[:, 0:24])), [("IW", 0, NC), ("pt16", 0, 24)], [("P1", 0, NT)])
-    for k in (3, 4):
-        pen_s("pen1", "P1", k)
-    quant("qu", "su", 0, 128, ("ub", 0, 512))
+    def to_list(out, row, col):
+        for r in range(4):
+            act((out, r, NT, 4), (row, r, NT, 4), scale=(col, r, r + 1))
+
+    quant("u", 0, 128, ("ub", 0, 512))
     do("v", lambda: V.tensor_copy(T.qur[:, 0:128].bitcast(dt.uint32), T.qu[:, 0:128].bitcast(dt.uint32).indirect(T.uo[:, 0:8])),
        [("qu", 0, 128), ("uo", 0, 8)], [("qur", 0, 128)])
     act(("sur", 0, 128), ("su", 0, 128), off=("uo", 0, 8))
-    pen_s("pen1", "P1", 5)
-    for k in (0, 1):
-        pen_v("pen1", "P1", k)
-    quant("qxk", "sxk", 0, NT + NC, ("xk", 0, XW + 4 * NC))
-    mm("p4", "qur", "sur", 0, "qxk", "sxk", 0, NT)
+    pen_v("pen1", "P1", 0)
+    pen_v("pen1", "P1", 1)
+    to_list("PM", "P1", "cm")
+    for k in range(PEN_S[0], 6):
+        pen_s("pen1", "P1", k)
+    ts(("r4", 0, NT), ("I4", 0, NT), 0.0, None, op_.not_equal)
+    ts(("cs", 0, 4), ("cm", 0, 4), 1.0 / GAP, None, op_.mult)
+    ts(("cn", 0, 4), ("R4", 0, 4), RP, BIG, op_.not_equal, op_.mult)
+    ts(("d16", 0, 12), ("c16", 0, 12), float(NT), None, op_.add)
+    fill(("A1", 4 * NC, 512), 0.0)
+    fill(("SC", 0, 4), 0.0)
+    quant("xk", 0, NT + NC, ("xk", 0, XW + 4 * NC))
+    mm(4, "ur", 0, "xk", 0, NT)
     for b in range(4):
-        mm("p%d" % b, "qE", "sE", 128 * b, "qxk", "sxk", 0, NT + NC)
-    pen_v("pen1", "P1", 2)
-    tt(("PM", 0, NT), ("P1", 0, NT), ("m4", 0, NT), op_.mult)
+        mm(b, "E", 128 * b, "xk", 0, NT + NC)
     scan(("PS", 0, NT), ("r4", 0, NT), ("PM", 0, NT), 0.0, op_.mult, op_.add)
-    ts(("Lf", 0, NC), ("PS", 3, NT, 4), 4.0, TP, op_.mult, op_.add)
     ts(("L41", 0, NC), ("PS", 3, NT, 4), 4.0, TP, op_.mult, op_.add)
-    copy(("adf", 0, 6), ("adI", 0, 6))
-    tt(("cma", 0, 6), ("c16", 0, 6), ("adf", 0, 6), op_.subtract)
-    copy(("adf2", 0, 6), ("c16", 6, 12))
-    copy(("adf2", 6, 12), ("adf", 0, 6))
-    tt(("cma2", 0, 12), ("c16", 0, 12), ("adf2", 0, 12), op_.subtract)
+    copy(("ea1", 6, 12), ("adI", 0, 6))
+    copy(("ea2", 12, 18), ("c16", 6, 12))
+    tt(("cma", 0, 6), ("c16", 0, 6), ("ea1", 6, 12), op_.subtract)
+    copy(("ea2", 18, 24), ("ea1", 6, 12))
+    tt(("cma2", 0, 12), ("c16", 0, 12), ("ea2", 12, 24), op_.subtract)
 
     for rnd in (0, 1):
         M = NC << rnd
         K = M // 16
-        pen, adf, cma = ("pen1", "adf", "cma") if rnd == 0 else ("pen2", "adf2", "cma2")
-        FG, GC, A = ("FG1", "GC1", "A1") if rnd == 0 else ("FG2", "GC2", "AB")
-        L4 = ("L41" if rnd == 0 else "L42", 0, NC)
-        AD = "ad1" if rnd == 0 else "ad2"
+        PL = NT + M
+        row, pen, cma = ("P1", "pen1", "cma") if rnd == 0 else ("P2", "pen2", "cma2")
+        ix, ea, qp, qb = ("ix1", "ea1", "qp1", "QB1") if rnd == 0 else ("ix2", "ea2", "qp2", "QB2")
+        FG, A, AD, L4 = ("FG1", "A1", "ad1", "L41") if rnd == 0 else ("FG2", "AB", "ad2", "L42")
+        B = ("B1", 0, 4 * M) if rnd == 0 else ("AB", 4 * M, 8 * M)
         h0 = 12 * rnd
+
+        def gc(t):
+            return ("GC1", t * NC, (t + 1) * NC) if rnd == 0 else ("GC2", t, 4 * M, 4)
+
+        if rnd == 1:
+            act(("GC2", 0, 4 * NC), ("A1", 0, 4 * NC), scale=0.5)
+            act(("GC2", 4 * NC, 8 * NC), ("B1", 0, 4 * NC), scale=0.5)
+            for t in range(4):
+                act(("FG2", t * PL + NT, t * PL + PL), gc(t))
+            for k in range(PEN_S[1], K):
+                pen_s(pen, row, k)
         fb = list(range(4))
-        for k in range(K):
-            w = ("W", k * NT, (k + 1) * NT)
-            if rnd == 1 and k < 7:
-                pen_v(pen, "P2", k)
-            tt(w, bank(4, NT), (pen, k * NT, (k + 1) * NT), op_.subtract)
-            scan(("MX", k * NT, (k + 1) * NT), w, w, -2.0 ** 80, op_.max, op_.max)
-            act(("JK", k * NT, (k + 1) * NT), ("MX", k * NT, (k + 1) * NT), AF.Sign, -1.0, ("MX", k * NT + NT - 1, k * NT + NT), ("idx", h0 + k, h0 + k + 1))
-            if fb and k >= 1 + 2 * rnd:
-                b = fb.pop(0)
-                n = NT + NC if rnd == 0 else NT
-                act((FG, b, 4 * n, 4), bank(b, n))
-                if not fb and rnd == 0:
-                    act(("GC1", 0, 4 * NC), ("FG1", XW, XW + 4 * NC))
-        H, E = ("hh", h0, h0 + K), ("ee", h0, h0 + K)
+
+        def evac():
+            b = fb.pop(0)
+            n = NT + NC if rnd == 0 else NT
+            act((FG, b * PL, b * PL + n), bank(b, n))
+            if rnd == 0:
+                act(gc(b), bank(b, PL, NT))
+
+        if rnd == 0:
+            evac()
+            evac()
+        for k in range(K + 1):
+            if k < K:
+                if rnd == 1 and k < PEN_S[1]:
+                    pen_v(pen, row, k)
+                tt(("W", k * NT, (k + 1) * NT), bank(4, NT), (pen, k * NT, (k + 1) * NT), op_.subtract)
+            if k > 0:
+                j = k - 1
+                w, m = ("W", j * NT, k * NT), ("MX", j * NT, k * NT)
+                scan(m, w, w, -2.0 ** 80, op_.max, op_.max)
+                act(("JK", j * NT, k * NT), m, AF.Sign, -1.0, ("MX", k * NT - 1, k * NT), (ix, j, k))
+                if fb and j >= 4 * rnd:
+                    evac()
+        H, QL, BL = ("hh", h0, h0 + K), (qb, 0, K), (qb, K, 2 * K)
         ts(H, ("MX", NT - 1, K * NT, NT), -2.0 ** 75, None, op_.is_le)
-        tt(("tb", h0, h0 + K), H, (cma, 0, K), op_.mult)
-        tt(("ap", h0, h0 + K), ("tb", h0, h0 + K), (adf, 0, K), op_.add)
+        tt((ea, 0, K), H, ("d16", 0, K), op_.mult)
+        tt((ix, K, 2 * K), H, (cma, 0, K), op_.mult)
+        tt((qp, 0, 2 * K), (ix, 0, 2 * K), (ea, 0, 2 * K), op_.add)
+        copy((qb, 0, 2 * K), (qp, 0, 2 * K))
+        bc = NC - BC[rnd]
         for t in range(4):
-            ts(("BL", 64 * rnd + 16 * t, 64 * rnd + 16 * t + K), ("ap", h0, h0 + K), 4.0, float(t), op_.mult, op_.add)
-        tt(E, H, ("d16", 0, K), op_.mult)
-        AH, B = (("FG2", XW, XW + 4 * M), ("B1", 0, 4 * M)) if rnd == 0 else (("AH2", 0, 4 * M), ("AB", 4 * M, 8 * M))
-        for t in range(4):
-            tt((B[0], B[1] + t, B[2], 4), (FG, XW, XW + 4 * M), (GC, t, 4 * M, 4), op_.add, ("BL", 64 * rnd + 16 * t, 64 * rnd + 16 * t + K))
-        act(("Bg", 0, XW), B, scale=0.5, off=L4)
-        QF = ("qf", h0, h0 + K)
-        tt(QF, ("idx", h0, h0 + K), E, op_.add)
-        for t in range(4):
-            ts(("QL", 80 * rnd + 16 * t, 80 * rnd + 16 * t + K), QF, 4.0, float(t), op_.mult, op_.add)
-        for t in range(4):
-            tt((A, t, 4 * M, 4), (FG, 0, XW + 4 * M), (GC, t, 4 * M, 4), op_.add, ("QL", 80 * rnd + 16 * t, 80 * rnd + 16 * t + K))
-        qa, sa, ra, rs = ("qa1", "sa1", "ra1", "rs1") if rnd == 0 else ("qa2", "sa2", "ra2", "rs2")
+            tt((A, t, 4 * M, 4), (FG, t * PL, t * PL + PL), gc(t), op_.add, QL)
+        act(("Ag", 0, 16 * bc), (A, 0, 4 * M), scale=0.5, off=(L4, 0, bc))
+        qa, ra = ("a1", "r1") if rnd == 0 else ("a2", "r2")
         nA = max(M, 128)
-        quant(qa, sa, 0, nA, (A, 0, 4 * nA))
-        wait("g", [hist[qa][-1][2]])
+        quant(qa, 0, nA, (A, 0, 4 * nA))
+        wait("g", [hist["q" + qa][-1][2]])
         arr = T.sem["arr%d" % (rnd + 1)]
-        g.remote_dma(T[ra][:, 0:nA].bitcast(dt.uint8), T[qa][:, 0:nA].bitcast(dt.uint8), arr, T.sem.sent, pid, rid, mask)
-        g.remote_dma(T[rs][:, 0:nA], T[sa][:, 0:nA], arr, T.sem.sent, pid, rid, mask)
+        g.remote_dma(T["q" + ra][:, 0:nA].bitcast(dt.uint8), T["q" + qa][:, 0:nA].bitcast(dt.uint8), arr, T.sem.sent, pid, rid, mask)
+        g.remote_dma(T["s" + ra][:, 0:nA], T["s" + qa][:, 0:nA], arr, T.sem.sent, pid, rid, mask)
         atok = ("arr%d" % (rnd + 1), 2 * n_eng, {})
-        note((ra, 0, nA), True, atok, "g")
-        note((rs, 0, nA), True, atok, "g")
-        final["arr%d" % (rnd + 1)] = atok
-        ts(AH, (A, 0, 4 * M), 0.5, None, op_.mult)
-        q0, s0, q1, s1 = ["%s%d" % (c, rnd + 1) for c in ("q0", "s0", "q1", "s1")]
-        tt(("VW", 0, XW), AH, (FG, 0, XW), op_.add, L4)
-        quant(q0, s0, 0, NT, ("VW", 0, XW))
-        mm("p5", "qur", "sur", 0, q0, s0, 0, NT)
-        copy(("QL", 80 * rnd + 64, 80 * rnd + 64 + K), QF)
-        do("v", lambda: V.tensor_copy(T[AD][:, 0:NT + M].indirect(T.QL[:, 80 * rnd + 64:80 * rnd + 64 + K]), T.IO4[:, NT:NT + M]),
-           [("IO4", NT, NT + M), ("QL", 80 * rnd + 64, 80 * rnd + 64 + K)], [(AD, 0, NT + M)])
+        note(("q" + ra, 0, nA), True, atok, "g")
+        note(("s" + ra, 0, nA), True, atok, "g")
+        final[atok[0]] = atok
+        for t in range(4):
+            tt((B[0], B[1] + t, B[2], 4), (FG, t * PL + NT, t * PL + PL), gc(t), op_.add, BL)
+        act(("Bg", 0, XW), B, scale=0.5, off=(L4, 0, NC))
+        if bc < NC:
+            ts(("Ag", 16 * bc, XW), (A, 0, 4 * M), 0.5, None, op_.mult, off=(L4, bc, NC))
+        put((AD, 0, PL), ("IO4", NT, PL), QL)
+        to_list("AM", AD, "cs")
+        for b in range(4):
+            tt(("VW", b, XW, 4), bank(b, NT), ("Ag", b, XW, 4), op_.add)
+        quant("0%d" % (rnd + 1), 0, NT, ("VW", 0, XW))
+        mm(5, "ur", 0, "0%d" % (rnd + 1), 0, NT)
+        for r in range(4):
+            act(("Z0", r, NT, 4), bank(5, NT, r, 4), AF.Identity, bias=("cn", r, r + 1))
+        act(("Zc", 0, NT), bank(5, NT))
         for b in range(4):
             tt(("VW", GAP + b, GAP + XW, 4), bank(b, NT), ("Bg", b, XW, 4), op_.add)
-        quant(q1, s1, 0, NT, ("VW", GAP, GAP + XW))
+        quant("1%d" % (rnd + 1), 0, NT, ("VW", GAP, GAP + XW))
         for b in range(4):
             pb = 7 if b % 2 == 0 else 4
-            mm("p%d" % pb, "wq", "wp", 128 * b, ra, rs, 0, nA)
+            mm(pb, "w", 128 * b, ra, 0, nA)
             act(("VW", XW + b, XW + 4 * M, 4), bank(pb, M), scale=0.03125)
-        act(("VW", GAP + XW, GAP + XW + 4 * M), ("VW", XW, XW + 4 * M))
-        mm("p6", "qur", "sur", 0, q1, s1, 0, NT)
-        tt(("Z0", 0, NT), bank(5, NT), ("dp", 0, NT), op_.add)
-        act(("Zc", 0, NT), bank(5, NT))
-        tt(("AM", 0, NT), (AD, 0, NT), ("m4s", 0, NT), op_.mult)
-        scan(("AS", 0, NT), ("r4", 0, NT), ("AM", 0, NT), 0.0, op_.mult, op_.add)
-        if rnd == 1:
-            quant("qv", "sv", 0, 128, ("vb", 0, 512))
-            quant("qb", "sb", 0, M, B)
-            mm("p0", "qv", "sv", 0, qa, sa, 0, M)
-            mm("p1", "qv", "sv", 0, "qb", "sb", 0, M)
-        tt(("CM", 0, NT), bank(6, NT), ("Z0", 0, NT), op_.is_gt)
-        scan(("SC", 0, NT), ("r4", 0, NT), ("CM", 0, NT), 0.0, op_.mult, op_.add)
-        tt(("T1", 0, NC), ("SC", 3, NT, 4), ("AS", 3, NT, 4), op_.add)
-        ts(("EL", 0, NC), ("T1", 0, NC), float(GAP), TP, op_.mult, op_.add)
-        X, qx, sx = ("X2", "qx2", "sx2") if rnd == 0 else ("X3", "qx3", "sx3")
-        cut = 44
-        act((X, 16 * cut, XW), ("VW", 0, WIN), off=("EL", cut, NC))
-        do("v", lambda: V.tensor_copy(T[X][:, 0:16 * cut], T.VW[:, 0:WIN].indirect(T.EL[:, 0:cut])), [("VW", 0, WIN), ("EL", 0, cut)], [(X, 0, 16 * cut)])
-        quant(qx, sx, 0, 4 * cut, (X, 0, 16 * cut))
-        quant(qx, sx, 4 * cut, NT, (X, 16 * cut, XW))
+        mm(6, "ur", 0, "1%d" % (rnd + 1), 0, NT)
         if rnd == 0:
-            mm("p4", "qur", "sur", 0, qx, sx, 0, NT)
-            for b in range(4):
-                mm("p%d" % b, "qE", "sE", 128 * b, qx, sx, 0, NT)
-            tt(("CR", 0, NT), bank(6, NT), ("Zc", 0, NT), op_.is_gt)
-            ts(("CS", 0, NT), ("CR", 0, NT), float(M), None, op_.mult)
+            ts(("Lf", 0, NC), ("PS", 3, NT, 4), 4.0, TP, op_.mult, op_.add)
+        else:
+            quant("v", 0, 128, ("vb", 0, 512))
+            quant("b", 0, M, B)
+            mm(0, "v", 0, qa, 0, M)
+            mm(1, "v", 0, "b", 0, M)
+            act(("zb", 0, M), bank(0, M))
+            act(("zb", M, 2 * M), bank(1, M))
+            store("y", "z", T.z[:], T.zb[:], ("zb", 0, NT))
+        tt(("CM", 0, NT), bank(6, NT), ("Z0", 0, NT), op_.is_gt)
+        scan(("SC", 4, NT + 4), ("CM", 0, NT), ("AM", 0, NT), 0.0, op_.add, op_.add)
+        tt(("T1", 0, NC), ("SC", 7, NT + 4, 4), ("SC", 3, NT, 4), op_.subtract)
+        ts(("EL", 0, NC), ("T1", 0, NC), float(GAP), TP, op_.mult, op_.add)
+        copy(("VW", GAP + XW, GAP + XW + 4 * M), ("VW", XW, XW + 4 * M))
+        X, qx = ("X2", "x2") if rnd == 0 else ("X3", "x3")
+        cut = CUT[rnd]
+        act((X, 16 * cut, XW), ("VW", 0, WIN), off=("EL", cut, NC))
+        pick((X, 0, 16 * cut), ("VW", 0, WIN), ("EL", 0, cut))
+        tt(("CR", 0, NT), bank(6, NT), ("Zc", 0, NT), op_.is_gt)
+        ts(("CS", 0, NT), ("CR", 0, NT), float(M), None, op_.mult)
+        if rnd == 0:
             tt(("P2", 0, NT), ("P1", 0, NT), ("CS", 0, NT), op_.add)
-            for k in range(7, 12):
-                pen_s("pen2", "P2", k)
-            act(("FG2", XW + 4 * NC, XW + 8 * NC), ("B1", 0, 4 * NC), scale=0.5)
-            act(("GC2", 0, 8 * NC), ("FG2", XW, XW + 8 * NC))
-            ts(("Lt", 0, NC), ("SC", 3, NT, 4), 4.0 * M, None, op_.mult)
+            quant(qx, 0, NT, (X, 0, XW))
+            mm(4, "ur", 0, qx, 0, NT)
+            for b in range(4):
+                mm(b, "E", 128 * b, qx, 0, NT)
+            ts(("Lt", 0, NC), ("T1", 0, NC), 1.0, 4.0 * M, op_.is_ge, op_.mult)
             tt(("Lg", 0, NC), ("Lt", 0, NC), ("Lf", 0, NC), op_.add)
             copy(("L42", 0, NC), ("Lg", 0, NC))
         else:
-            act(("zb", 0, M), bank(0, M))
-            act(("zb", M, 2 * M), bank(1, M))
-            do("y", lambda: g.sync.dma_start(T.z[:], T.zb[:]), [("zb", 0, NT)], [], dma="z")
-            mm("p7", "qv", "sv", 0, qx, sx, 0, NT)
-            act(("yb", 0, NT), bank(7, NT))
-            do("s", lambda: S.dma_start(T.y[:], T.yb[:]), [("yb", 0, NT)], [], dma="y")
-            do("y", lambda: g.sync.dma_start(T.oc[:], T.qx3[:, 0:NT].bitcast(dt.uint8)), [("qx3", 0, NT)], [], dma="oc")
-            for i in range(4):
-                do("y", lambda: g.sync.dma_start(T.osc[4 * i:4 * i + 4, 0:NT], T.sx3[32 * i:32 * i + 4, 0:NT]), [("sx3", 0, NT)], [], dma="o%d" % i)
-            tt(("CR", 0, NT), bank(6, NT), ("Zc", 0, NT), op_.is_gt)
-            ts(("CS", 0, NT), ("CR", 0, NT), float(M), None, op_.mult)
+            c = NT // 2
+            quant(qx, 0, c, (X, 0, 4 * c))
+            quant(qx, c, NT, (X, 4 * c, XW))
+            mm(7, "v", 0, qx, 0, c)
+            mm(4, "v", 0, qx, c, NT)
+            act(("yb", 0, c), bank(7, c))
+            act(("yb", c, NT), bank(4, NT - c))
+            store("s", "y0", T.y[:, 0:c], T.yb[:, 0:c], ("yb", 0, c))
+            store("s", "y1", T.y[:, c:NT], T.yb[:, c:NT], ("yb", c, NT))
             tt(("opr", 0, NT), ("P2", 0, NT), ("CS", 0, NT), op_.add)
-            do("y", lambda: g.sync.dma_start(T.op[:], T.opr[0:128:16, 0:NT]), [("opr", 0, NT)], [], dma="op")
+            store("y", "oc", T.oc[:], T.qx3[:, 0:NT].bitcast(dt.uint8), ("qx3", 0, NT))
+            for i in range(4):
+                store("y", "o%d" % i, T.osc[4 * i:4 * i + 4, 0:NT], T.sx3[32 * i:32 * i + 4, 0:NT], ("sx3", 0, NT))
+            store("y", "op", T.op[:], T.opr[0:128:16, 0:NT], ("opr", 0, NT))
     g.wait_ge(T.sem.sent, 4 * n_eng)
     wait("y", list(final.values()))

@@ -6,9 +6,10 @@ XW = 4 * NT
 GAP = 4096
 WIN = GAP + XW + 4 * 2 * NC
 BIG = 2.0 ** 90
-CUT = (20, 36)
-PEN_S = (2, 3)
-BC = (24, 0)
+CUT = (20, 28)
+CUT2 = (68, 64)
+PEN_S = (2, 2)
+BC = (24, 4)
 
 
 def _sb(n, d):
@@ -16,13 +17,13 @@ def _sb(n, d):
 
 
 SCRATCH = {
-    "xk": _sb(XW + 4 * NC, BF16), "ub": _sb(512, BF16), "vb": _sb(512, BF16), "ptI": _sb(24, I32), "adI": _sb(6, I32),
-    "half": _sb(128, BF16), "dg": _sb(128, BF16), "ET": _sb(2048, BF16),
+    "xb": _sb(XW, BF16), "kb": _sb(512, BF16), "ub": _sb(512, BF16), "vb": _sb(512, BF16), "ptI": _sb(24, I32), "adI": _sb(6, I32),
+    "half": _sb(128, BF16), "dg": _sb(128, BF16), "ZE": _sb(516, BF16),
     "pi": _sb(1, I32), "pj": _sb(4, I32), "pf": _sb(4, F32), "IW": _sb(NC, F32), "R4": _sb(4, F32), "K16": _sb(12, F32), "I4": _sb(NT, BF16),
     "cm": _sb(4, F32), "cs": _sb(4, F32), "cn": _sb(4, F32), "r4": _sb(NT, BF16),
     "c16": _sb(12, F32), "d16": _sb(12, F32), "nb": _sb(12, F32), "uoI": _sb(8, I32), "uo": _sb(8, U16), "IO4": _sb(NT + 2 * NC, F32),
     "ad1": _sb(NT + NC, F32), "ad2": _sb(NT + 2 * NC, F32),
-    "pt16": _sb(24, U16), "P1": _sb(NT, BF16), "P2": _sb(NT, BF16), "PM": _sb(NT, BF16), "PS": _sb(NT, BF16),
+    "pt16": _sb(24, U16), "P1": _sb(NT, BF16), "P2": _sb(NT, BF16), "P1m": _sb(NT, BF16), "P2m": _sb(NT, F32), "PM": _sb(NT, BF16), "PS": _sb(NT, BF16),
     "Lf": _sb(NC, F32), "L41": _sb(NC, U16), "Lt": _sb(NC, F32), "Lg": _sb(NC, F32), "L42": _sb(NC, U16),
     "pen1": _sb(6 * NT, BF16), "pen2": _sb(12 * NT, BF16), "W": _sb(12 * NT, F32), "MX": _sb(12 * NT, F32), "JK": _sb(12 * NT, BF16),
     "cma": _sb(12, F32), "cma2": _sb(12, F32), "hh": _sb(24, F32),
@@ -35,12 +36,12 @@ SCRATCH = {
     "AM": _sb(NT, F32), "T1": _sb(NC, F32), "EL": _sb(NC, U16), "opr": _sb(NT, F32),
     "yb": _sb(NT, F32), "zb": _sb(NT, F32),
 }
-for _n, _w in (("w", 512), ("xk", NT + NC), ("x2", NT), ("x3", NT), ("u", 128), ("ur", 128), ("v", 128), ("E", 512), ("a1", 128), ("a2", 192),
+for _n, _w in (("w", 512), ("xk", NT + 128), ("x2", NT), ("x3", NT), ("u", 128), ("ur", 128), ("v", 128), ("E", 512), ("a1", 128), ("a2", 192),
                ("r1", 128), ("r2", 192), ("01", NT), ("11", NT), ("02", NT), ("12", NT), ("b", 192)):
     SCRATCH["q" + _n], SCRATCH["s" + _n] = _sb(_w, F8), _sb(_w, U8)
 for _i in range(8):
     SCRATCH["p%d" % _i] = ("psum", [128, 512], F32)
-_DMAS = ["pt", "x", "k", "u", "ad", "w", "ws", "v", "op", "y0", "y1", "z", "oc", "o0", "o1", "o2", "o3"]
+_DMAS = ["pt", "x", "k", "u", "ad", "w", "ws", "v", "op", "y0", "y1", "z", "oc", "oc1", "o0", "o1", "o2", "o3"]
 SEMAPHORES = ["cv", "cs", "ct", "cg"] + ["d_" + n for n in _DMAS] + ["arr1", "arr2", "sent"]
 
 
@@ -138,9 +139,11 @@ def rank_program(g, core, T, topo):
 
     def act(out, in_, func=AF.Copy, scale=1.0, bias=None, acc=None, off=None):
         reads, writes, kw, src = [in_], [out], {}, ap(in_)
-        if bias is not None:
+        if isinstance(bias, tuple):
             reads.append(bias)
             kw["bias"] = ap(bias)
+        elif bias is not None:
+            kw["bias"] = bias
         if isinstance(scale, tuple):
             reads.append(scale)
             kw["scale"] = ap(scale)
@@ -173,8 +176,8 @@ def rank_program(g, core, T, topo):
 
     load("y", "pt", ("ptI", 0, 24), T.pt[:])
     load("s", "u", ("ub", 0, 512), T.u[:])
-    load("y", "x", ("xk", 0, XW), T.x[:])
-    load("s", "k", ("xk", XW, XW + 4 * NC), T.k[:])
+    load("y", "x", ("xb", 0, XW), T.x[:])
+    load("s", "k", ("kb", 0, 4 * NC), T.k[:])
     load("y", "ad", ("adI", 0, 6), T.ad[:])
     load("y", "w", ("qw", 0, 512), T.wc[:], bc=True)
     load("y", "ws", ("sw", 0, 512), T.ws[:])
@@ -188,9 +191,8 @@ def rank_program(g, core, T, topo):
     do("g", lambda: g.affine_select(T.dg[:], T.half[:], [[-1, 128]], op_.is_equal, 0.0, 0, 1), [("half", 0, 128)], [("dg", 0, 128)])
     iota(("uoI", 0, 8), [[16, 8]])
     iota(("I4", 0, NT), [[0, NT // 4], [1, 4]])
-    fill(("ET", 0, 2048), 0.0)
-    for b in range(4):
-        act(("ET", 512 * b + b, 512 * b + 512, 4), ("dg", 0, 128))
+    fill(("ZE", 0, 516), 0.0)
+    act(("ZE", 3, 515, 4), ("dg", 0, 128))
     iota(("IO4", 0, NT + 2 * NC), [[4, NT + 2 * NC]])
     iota(("ad1", 0, NT), [[4, NT]])
     iota(("VW", XW + 4 * NC, GAP), [[0, GAP - XW - 4 * NC]])
@@ -205,8 +207,13 @@ def rank_program(g, core, T, topo):
     ts(("cm", 0, 4), ("R4", 0, 4), RP, None, op_.is_equal)
     ts(("nb", 0, 12), ("c16", 0, 12), -BIG, None, op_.mult)
     copy(("uo", 0, 8), ("uoI", 0, 8))
+    ts(("cs", 0, 4), ("cm", 0, 4), 1.0 / GAP, None, op_.mult)
+    ts(("cn", 0, 4), ("R4", 0, 4), RP, BIG, op_.not_equal, op_.mult)
+    ts(("d16", 0, 12), ("c16", 0, 12), float(NT), None, op_.add)
+    fill(("A1", 4 * NC, 512), 0.0)
+    fill(("SC", 0, 4), 0.0)
+    fill(("kb", 4 * NC, 512), 0.0)
     copy(("pt16", 0, 24), ("ptI", 0, 24))
-    quant("E", 0, 512, ("ET", 0, 2048))
     pick(("P1", 0, NT), ("IW", 0, NC), ("pt16", 0, 24))
 
     def pen_v(pen, row, k):
@@ -219,32 +226,25 @@ def rank_program(g, core, T, topo):
         for r in range(4):
             act((out, r, NT, 4), (row, r, NT, 4), scale=(col, r, r + 1))
 
+    to_list("PM", "P1", "cm")
     quant("u", 0, 128, ("ub", 0, 512))
     do("v", lambda: V.tensor_copy(T.qur[:, 0:128].bitcast(dt.uint32), T.qu[:, 0:128].bitcast(dt.uint32).indirect(T.uo[:, 0:8])),
        [("qu", 0, 128), ("uo", 0, 8)], [("qur", 0, 128)])
     act(("sur", 0, 128), ("su", 0, 128), off=("uo", 0, 8))
     pen_v("pen1", "P1", 0)
     pen_v("pen1", "P1", 1)
-    to_list("PM", "P1", "cm")
     for k in range(PEN_S[0], 6):
         pen_s("pen1", "P1", k)
     ts(("r4", 0, NT), ("I4", 0, NT), 0.0, None, op_.not_equal)
-    ts(("cs", 0, 4), ("cm", 0, 4), 1.0 / GAP, None, op_.mult)
-    ts(("cn", 0, 4), ("R4", 0, 4), RP, BIG, op_.not_equal, op_.mult)
-    ts(("d16", 0, 12), ("c16", 0, 12), float(NT), None, op_.add)
-    fill(("A1", 4 * NC, 512), 0.0)
-    fill(("SC", 0, 4), 0.0)
-    quant("xk", 0, NT + NC, ("xk", 0, XW + 4 * NC))
-    mm(4, "ur", 0, "xk", 0, NT)
-    for b in range(4):
-        mm(b, "E", 128 * b, "xk", 0, NT + NC)
     scan(("PS", 0, NT), ("r4", 0, NT), ("PM", 0, NT), 0.0, op_.mult, op_.add)
     ts(("L41", 0, NC), ("PS", 3, NT, 4), 4.0, TP, op_.mult, op_.add)
-    copy(("ea1", 6, 12), ("adI", 0, 6))
     copy(("ea2", 12, 18), ("c16", 6, 12))
-    tt(("cma", 0, 6), ("c16", 0, 6), ("ea1", 6, 12), op_.subtract)
-    copy(("ea2", 18, 24), ("ea1", 6, 12))
-    tt(("cma2", 0, 12), ("c16", 0, 12), ("ea2", 12, 24), op_.subtract)
+    quant("xk", 0, NT, ("xb", 0, XW))
+    mm(4, "ur", 0, "xk", 0, NT)
+    for b in range(4):
+        quant("E", 128 * b, 128 * b + 128, ("ZE", 3 - b, 515 - b))
+    for b in range(4):
+        mm(b, "E", 128 * b, "xk", 0, NT)
 
     for rnd in (0, 1):
         M = NC << rnd
@@ -260,8 +260,6 @@ def rank_program(g, core, T, topo):
             return ("GC1", t * NC, (t + 1) * NC) if rnd == 0 else ("GC2", t, 4 * M, 4)
 
         if rnd == 1:
-            act(("GC2", 0, 4 * NC), ("A1", 0, 4 * NC), scale=0.5)
-            act(("GC2", 4 * NC, 8 * NC), ("B1", 0, 4 * NC), scale=0.5)
             for t in range(4):
                 act(("FG2", t * PL + NT, t * PL + PL), gc(t))
             for k in range(PEN_S[1], K):
@@ -270,10 +268,13 @@ def rank_program(g, core, T, topo):
 
         def evac():
             b = fb.pop(0)
-            n = NT + NC if rnd == 0 else NT
-            act((FG, b * PL, b * PL + n), bank(b, n))
-            if rnd == 0:
-                act(gc(b), bank(b, PL, NT))
+            act((FG, b * PL, b * PL + NT), bank(b, NT))
+
+        def cells(b):
+            pb = 5 + b % 3
+            mm(pb, "E", 128 * b, "xk", NT, NT + 128)
+            act((FG, b * PL + NT, b * PL + PL), bank(pb, NC))
+            act(gc(b), bank(pb, NC))
 
         if rnd == 0:
             evac()
@@ -283,6 +284,10 @@ def rank_program(g, core, T, topo):
                 if rnd == 1 and k < PEN_S[1]:
                     pen_v(pen, row, k)
                 tt(("W", k * NT, (k + 1) * NT), bank(4, NT), (pen, k * NT, (k + 1) * NT), op_.subtract)
+            if rnd == 0 and k == 0:
+                quant("xk", NT, NT + 128, ("kb", 0, 512))
+            if rnd == 0 and k == 5:
+                copy(("ea1", 6, 12), ("adI", 0, 6))
             if k > 0:
                 j = k - 1
                 w, m = ("W", j * NT, k * NT), ("MX", j * NT, k * NT)
@@ -290,10 +295,17 @@ def rank_program(g, core, T, topo):
                 act(("JK", j * NT, k * NT), m, AF.Sign, -1.0, ("MX", k * NT - 1, k * NT), (ix, j, k))
                 if fb and j >= 4 * rnd:
                     evac()
+                elif rnd == 0 and j in (2, 3):
+                    cells(2 * (j - 2))
+                    cells(2 * (j - 2) + 1)
         H, QL, BL = ("hh", h0, h0 + K), (qb, 0, K), (qb, K, 2 * K)
         ts(H, ("MX", NT - 1, K * NT, NT), -2.0 ** 75, None, op_.is_le)
+        if rnd == 0:
+            tt(("cma", 0, 6), ("c16", 0, 6), ("ea1", 6, 12), op_.subtract)
         tt((ea, 0, K), H, ("d16", 0, K), op_.mult)
         tt((ix, K, 2 * K), H, (cma, 0, K), op_.mult)
+        if rnd == 1:
+            copy(("L42", 0, NC), ("Lg", 0, NC))
         tt((qp, 0, 2 * K), (ix, 0, 2 * K), (ea, 0, 2 * K), op_.add)
         copy((qb, 0, 2 * K), (qp, 0, 2 * K))
         bc = NC - BC[rnd]
@@ -314,10 +326,13 @@ def rank_program(g, core, T, topo):
         for t in range(4):
             tt((B[0], B[1] + t, B[2], 4), (FG, t * PL + NT, t * PL + PL), gc(t), op_.add, BL)
         act(("Bg", 0, XW), B, scale=0.5, off=(L4, 0, NC))
-        if bc < NC:
-            ts(("Ag", 16 * bc, XW), (A, 0, 4 * M), 0.5, None, op_.mult, off=(L4, bc, NC))
+        ts(("Ag", 16 * bc, XW), (A, 0, 4 * M), 0.5, None, op_.mult, off=(L4, bc, NC))
         put((AD, 0, PL), ("IO4", NT, PL), QL)
         to_list("AM", AD, "cs")
+        if rnd == 0:
+            act(("P1m", 0, NT), ("P1", 0, NT), bias=-256.0)
+        else:
+            act(("P2m", 0, NT), ("P2", 0, NT), bias=-512.0)
         for b in range(4):
             tt(("VW", b, XW, 4), bank(b, NT), ("Ag", b, XW, 4), op_.add)
         quant("0%d" % (rnd + 1), 0, NT, ("VW", 0, XW))
@@ -327,16 +342,23 @@ def rank_program(g, core, T, topo):
         act(("Zc", 0, NT), bank(5, NT))
         for b in range(4):
             tt(("VW", GAP + b, GAP + XW, 4), bank(b, NT), ("Bg", b, XW, 4), op_.add)
+        if rnd == 1:
+            quant("v", 0, 128, ("vb", 0, 512))
         quant("1%d" % (rnd + 1), 0, NT, ("VW", GAP, GAP + XW))
         for b in range(4):
             pb = 7 if b % 2 == 0 else 4
             mm(pb, "w", 128 * b, ra, 0, nA)
             act(("VW", XW + b, XW + 4 * M, 4), bank(pb, M), scale=0.03125)
-        mm(6, "ur", 0, "1%d" % (rnd + 1), 0, NT)
+            if b == 1:
+                mm(6, "ur", 0, "1%d" % (rnd + 1), 0, NT)
+        act(("VW", GAP + XW, GAP + XW + 4 * M), ("VW", XW, XW + 4 * M))
         if rnd == 0:
+            copy(("ea2", 18, 24), ("ea1", 6, 12))
             ts(("Lf", 0, NC), ("PS", 3, NT, 4), 4.0, TP, op_.mult, op_.add)
+            tt(("cma2", 0, 12), ("c16", 0, 12), ("ea2", 12, 24), op_.subtract)
+            act(("GC2", 0, 4 * NC), ("A1", 0, 4 * NC), scale=0.5)
+            act(("GC2", 4 * NC, 8 * NC), ("B1", 0, 4 * NC), scale=0.5)
         else:
-            quant("v", 0, 128, ("vb", 0, 512))
             quant("b", 0, M, B)
             mm(0, "v", 0, qa, 0, M)
             mm(1, "v", 0, "b", 0, M)
@@ -347,34 +369,35 @@ def rank_program(g, core, T, topo):
         scan(("SC", 4, NT + 4), ("CM", 0, NT), ("AM", 0, NT), 0.0, op_.add, op_.add)
         tt(("T1", 0, NC), ("SC", 7, NT + 4, 4), ("SC", 3, NT, 4), op_.subtract)
         ts(("EL", 0, NC), ("T1", 0, NC), float(GAP), TP, op_.mult, op_.add)
-        copy(("VW", GAP + XW, GAP + XW + 4 * M), ("VW", XW, XW + 4 * M))
         X, qx = ("X2", "x2") if rnd == 0 else ("X3", "x3")
-        cut = CUT[rnd]
-        act((X, 16 * cut, XW), ("VW", 0, WIN), off=("EL", cut, NC))
+        hc, c, cut, cut2 = NC // 2, NT // 2, CUT[rnd], CUT2[rnd]
+        act((X, 16 * cut, 16 * hc), ("VW", 0, WIN), off=("EL", cut, hc))
+        act((X, 16 * cut2, XW), ("VW", 0, WIN), off=("EL", cut2, NC))
         pick((X, 0, 16 * cut), ("VW", 0, WIN), ("EL", 0, cut))
+        pick((X, 16 * hc, 16 * cut2), ("VW", 0, WIN), ("EL", hc, cut2))
+        quant(qx, 0, c, (X, 0, 4 * c))
         tt(("CR", 0, NT), bank(6, NT), ("Zc", 0, NT), op_.is_gt)
-        ts(("CS", 0, NT), ("CR", 0, NT), float(M), None, op_.mult)
+        if rnd == 1:
+            mm(7, "v", 0, qx, 0, c)
+            store("y", "oc", T.oc[:, 0:4 * c], T.qx3[:, 0:c].bitcast(dt.uint8), ("qx3", 0, c))
+            quant(qx, c, NT, (X, 4 * c, XW))
+            mm(4, "v", 0, qx, c, NT)
+        ts(("CS", 0, NT), ("CR", 0, NT), float(M), 256.0 if rnd == 0 else 512.0, op_.mult, op_.add)
         if rnd == 0:
-            tt(("P2", 0, NT), ("P1", 0, NT), ("CS", 0, NT), op_.add)
-            quant(qx, 0, NT, (X, 0, XW))
+            scan(("P2", 0, NT), ("CS", 0, NT), ("P1m", 0, NT), 0.0, op_.max, op_.add)
+            quant(qx, c, NT, (X, 4 * c, XW))
             mm(4, "ur", 0, qx, 0, NT)
             for b in range(4):
                 mm(b, "E", 128 * b, qx, 0, NT)
             ts(("Lt", 0, NC), ("T1", 0, NC), 1.0, 4.0 * M, op_.is_ge, op_.mult)
             tt(("Lg", 0, NC), ("Lt", 0, NC), ("Lf", 0, NC), op_.add)
-            copy(("L42", 0, NC), ("Lg", 0, NC))
         else:
-            c = NT // 2
-            quant(qx, 0, c, (X, 0, 4 * c))
-            quant(qx, c, NT, (X, 4 * c, XW))
-            mm(7, "v", 0, qx, 0, c)
-            mm(4, "v", 0, qx, c, NT)
-            act(("yb", 0, c), bank(7, c))
+            copy(("yb", 0, c), bank(7, c))
+            store("y", "y0", T.y[:, 0:c], T.yb[:, 0:c], ("yb", 0, c))
             act(("yb", c, NT), bank(4, NT - c))
-            store("s", "y0", T.y[:, 0:c], T.yb[:, 0:c], ("yb", 0, c))
             store("s", "y1", T.y[:, c:NT], T.yb[:, c:NT], ("yb", c, NT))
-            tt(("opr", 0, NT), ("P2", 0, NT), ("CS", 0, NT), op_.add)
-            store("y", "oc", T.oc[:], T.qx3[:, 0:NT].bitcast(dt.uint8), ("qx3", 0, NT))
+            store("y", "oc1", T.oc[:, 4 * c:4 * NT], T.qx3[:, c:NT].bitcast(dt.uint8), ("qx3", c, NT))
+            scan(("opr", 0, NT), ("CS", 0, NT), ("P2m", 0, NT), 0.0, op_.max, op_.add)
             for i in range(4):
                 store("y", "o%d" % i, T.osc[4 * i:4 * i + 4, 0:NT], T.sx3[32 * i:32 * i + 4, 0:NT], ("sx3", 0, NT))
             store("y", "op", T.op[:], T.opr[0:128:16, 0:NT], ("opr", 0, NT))

from concourse.mybir import dt, AluOpType, ActivationFunctionType

F32, BF16, I32, U16, F8, U8 = "float32", "bfloat16", "int32", "uint16", "float8_e4m3fn_x4", "uint8"
NT, NC = 384, 96
XW = 4 * NT
GAP = 4096
WIN = GAP + XW + 4 * 2 * NC
BIG = 2.0 ** 90
CUT = (20, 28)
CUT2 = (68, 64)
PEN_S = (2, 2)
BC = (24, 4)


def _sb(n, d):
    return ("sbuf", [128, n], d)


SCRATCH = {
    "xb": _sb(XW, BF16), "kb": _sb(512, BF16), "ub": _sb(512, BF16), "vb": _sb(512, BF16), "ptI": _sb(24, I32), "adI": _sb(6, I32),
    "half": _sb(128, BF16), "dg": _sb(128, BF16), "ZE": _sb(516, BF16),
    "pi": _sb(1, I32), "pj": _sb(4, I32), "pf": _sb(4, F32), "IW": _sb(NC, F32), "R4": _sb(4, F32), "K16": _sb(12, F32), "I4": _sb(NT, BF16),
    "cm": _sb(4, F32), "cs": _sb(4, F32), "cn": _sb(4, F32), "r4": _sb(NT, BF16),
    "c16": _sb(12, F32), "d16": _sb(12, F32), "nb": _sb(12, F32), "uoI": _sb(8, I32), "uo": _sb(8, U16), "IO4": _sb(NT + 2 * NC, F32),
    "ad1": _sb(NT + NC, F32), "ad2": _sb(NT + 2 * NC, F32),
    "pt16": _sb(24, U16), "P1": _sb(NT, BF16), "P2": _sb(NT, BF16), "P1m": _sb(NT, BF16), "P2m": _sb(NT, F32), "PM": _sb(NT, BF16), "PS": _sb(NT, BF16),
    "Lf": _sb(NC, F32), "L41": _sb(NC, U16), "Lt": _sb(NC, F32), "Lg": _sb(NC, F32), "L42": _sb(NC, U16),
    "pen1": _sb(6 * NT, BF16), "pen2": _sb(12 * NT, BF16), "W": _sb(12 * NT, F32), "MX": _sb(12 * NT, F32), "JK": _sb(12 * NT, BF16),
    "cma": _sb(12, F32), "cma2": _sb(12, F32), "hh": _sb(24, F32),
    "ix1": _sb(12, F32), "ix2": _sb(24, F32), "ea1": _sb(12, F32), "ea2": _sb(24, F32), "qp1": _sb(12, F32), "qp2": _sb(24, F32),
    "QB1": _sb(12, U16), "QB2": _sb(24, U16),
    "FG1": _sb(4 * (NT + NC), BF16), "FG2": _sb(4 * (NT + 2 * NC), BF16), "GC1": _sb(4 * NC, BF16), "GC2": _sb(8 * NC, BF16),
    "A1": _sb(512, BF16), "B1": _sb(4 * NC, BF16), "AB": _sb(XW, BF16), "Ag": _sb(XW, BF16), "Bg": _sb(XW, BF16),
    "VW": _sb(WIN, BF16), "X2": _sb(XW, BF16), "X3": _sb(XW, BF16),
    "Z0": _sb(NT, F32), "Zc": _sb(NT, F32), "CM": _sb(NT, BF16), "CR": _sb(NT, BF16), "CS": _sb(NT, BF16), "SC": _sb(NT + 4, F32),
    "AM": _sb(NT, F32), "T1": _sb(NC, F32), "EL": _sb(NC, U16), "opr": _sb(NT, F32),
    "yb": _sb(NT, F32), "zb": _sb(NT, F32),
}
for _n, _w in (("w", 512), ("xk", NT + 128), ("x2", NT), ("x3", NT), ("u", 128), ("ur", 128), ("v", 128), ("E", 512), ("a1", 128), ("a2", 192),
               ("r1", 128), ("r2", 192), ("01", NT), ("11", NT), ("02", NT), ("12", NT), ("b", 192)):
    SCRATCH["q" + _n], SCRATCH["s" + _n] = _sb(_w, F8), _sb(_w, U8)
for _i in range(8):
    SCRATCH["p%d" % _i] = ("psum", [128, 512], F32)
_DMAS = ["pt", "x", "k", "u", "ad", "w", "ws", "v", "op", "y0", "y1", "z", "oc", "oc1", "o0", "o1", "o2", "o3"]
SEMAPHORES = ["cv", "cs", "ct", "cg"] + ["d_" + n for n in _DMAS] + ["arr1", "arr2", "sent"]


def rank_program(g, core, T, topo):
    rank = T.rank_of(core)
    if rank is None:
        return
    nxt = T.cores[(rank + 1) % len(T.cores)]
    rid, pid = topo.addr(nxt)[:2]
    engs = topo.engines(core, nxt)[:8]
    mask, n_eng = sum(1 << e for e in engs), len(engs)
    Q = {"v": g.vector, "s": g.scalar, "t": g.tensor, "g": g, "y": g.sync}
    op_, AF = AluOpType, ActivationFunctionType
    V, S = g.vector, g.scalar

    count, known, hist, final = {}, {e: {} for e in Q}, {}, {}

    def ap(r):
        return T[r[0]][:, r[1]:r[2]] if len(r) < 4 or r[3] == 1 else T[r[0]][:, r[1]:r[2]:r[3]]

    def meet(a, b):
        if a[2] <= b[1] or b[2] <= a[1]:
            return False
        sa, sb = (a[3] if len(a) > 3 else 1), (b[3] if len(b) > 3 else 1)
        return not (sa == sb and sa > 1 and a[1] % sa != b[1] % sa)

    def wait(e, toks):
        best = {}
        for t in toks:
            if t[0] not in best or best[t[0]][1] < t[1]:
                best[t[0]] = t
        for t in sorted(best.values(), key=lambda t: -len(t[2])):
            if known[e].get(t[0], 0) >= t[1]:
                continue
            Q[e].wait_ge(T.sem[t[0]], t[1])
            for k, v in t[2].items():
                known[e][k] = max(known[e].get(k, 0), v)
            known[e][t[0]] = max(known[e].get(t[0], 0), t[1])

    def note(r, wr, tok, e):
        hist.setdefault(r[0], []).append((r, wr, tok, e))

    def do(e, fn, reads, writes, dma=None):
        toks = []
        for rs, wr in ((reads, False), (writes, True)):
            for r in rs:
                ps = SCRATCH[r[0]][0] == "psum"
                for (o, ow, tok, oe) in hist.get(r[0], []):
                    if (wr or ow or (ps and oe != e)) and (ps or meet(r, o)):
                        toks.append(tok)
        wait(e, toks)
        ins = fn()
        sem, n = ("d_" + dma, 16) if dma is not None else ("c" + e, 1)
        count[sem] = count.get(sem, 0) + n
        ins.then_inc(T.sem[sem], n)
        tok = (sem, count[sem], dict(known[e]))
        final[sem] = tok
        for r in reads:
            note(r, False, tok, e)
        for r in writes:
            note(r, True, tok, e)

    def load(e, name, dst, src, bc=False):
        d = ap(dst).bitcast(dt.uint8) if bc else ap(dst)
        do(e, lambda: Q[e].dma_start(d, src), [], [dst], dma=name)

    def store(e, name, dst, src, rd):
        do(e, lambda: Q[e].dma_start(dst, src), [rd], [], dma=name)

    def copy(out, in_):
        do("v", lambda: V.tensor_copy(ap(out), ap(in_)), [in_], [out])

    def ts(out, in0, s1, s2, o0, o1=None, off=None):
        reads = [in0] + [s for s in (s1, s2, off) if isinstance(s, tuple)]
        a = ap(s1) if isinstance(s1, tuple) else s1
        b = ap(s2) if isinstance(s2, tuple) else s2
        src = ap(in0) if off is None else ap(in0).indirect(ap(off))
        if o1 is None:
            do("v", lambda: V.tensor_scalar(ap(out), src, a, None, o0), reads, [out])
        else:
            do("v", lambda: V.tensor_scalar(ap(out), src, a, b, o0, o1), reads, [out])

    def tt(out, in0, in1, o, off=None):
        src = ap(in0) if off is None else ap(in0).indirect(ap(off))
        do("v", lambda: V.tensor_tensor(ap(out), src, ap(in1), o), [in0, in1] + ([] if off is None else [off]), [out])

    def pick(out, in_, off):
        do("v", lambda: V.tensor_copy(ap(out), ap(in_).indirect(ap(off))), [in_, off], [out])

    def put(out, in_, off):
        do("v", lambda: V.tensor_copy(ap(out).indirect(ap(off)), ap(in_)), [in_, off], [out])

    def scan(out, d0, d1, init, o0, o1):
        do("v", lambda: V.tensor_tensor_scan(ap(out), ap(d0), ap(d1), init, o0, o1), [d0, d1], [out])

    def act(out, in_, func=AF.Copy, scale=1.0, bias=None, acc=None, off=None):
        reads, writes, kw, src = [in_], [out], {}, ap(in_)
        if isinstance(bias, tuple):
            reads.append(bias)
            kw["bias"] = ap(bias)
        elif bias is not None:
            kw["bias"] = bias
        if isinstance(scale, tuple):
            reads.append(scale)
            kw["scale"] = ap(scale)
        elif scale != 1.0:
            kw["scale"] = scale
        if acc is not None:
            writes.append(acc)
            kw["accum_out"] = ap(acc)
        if off is not None:
            reads.append(off)
            src = src.indirect(ap(off))
        do("s", lambda: S.activation(ap(out), src, func, **kw), reads, writes)

    def quant(n, a, b, src):
        do("v", lambda: V.quantize_mx(T["q" + n][:, a:b], T["s" + n][:, a:b], ap(src)), [src], [("q" + n, a, b), ("s" + n, a, b)])

    def mm(pb, ln, la, rn, ra, rb):
        lq, ls, rq, rs = ("q" + ln, la, la + 128), ("s" + ln, la, la + 128), ("q" + rn, ra, rb), ("s" + rn, ra, rb)
        do("t", lambda: g.tensor.matmul_mx(T["p%d" % pb][:, 0:rb - ra], ap(lq), ap(ls), ap(rq), ap(rs), True, True), [lq, ls, rq, rs], [("p%d" % pb, 0, 512)])

    def bank(i, n, a=0, st=1):
        return ("p%d" % i, a, n, st)

    def iota(out, pattern, base=0, cm=0):
        kw = {} if SCRATCH[out[0]][2] == I32 else {"allow_small_or_imprecise_dtypes": True}
        do("g", lambda: g.iota(ap(out), pattern, base, cm, **kw), [], [out])

    def fill(out, c):
        do("v", lambda: V.memset(ap(out), c), [], [out])

    load("y", "pt", ("ptI", 0, 24), T.pt[:])
    load("s", "u", ("ub", 0, 512), T.u[:])
    load("y", "x", ("xb", 0, XW), T.x[:])
    load("s", "k", ("kb", 0, 4 * NC), T.k[:])
    load("y", "ad", ("adI", 0, 6), T.ad[:])
    load("y", "w", ("qw", 0, 512), T.wc[:], bc=True)
    load("y", "ws", ("sw", 0, 512), T.ws[:])
    load("y", "v", ("vb", 0, 512), T.v[:])

    fill(("half", 0, 128), 0.5)
    iota(("pi", 0, 1), [[0, 1]], 0, 1)
    iota(("IW", 0, NC), [[1, NC]])
    iota(("K16", 0, 12), [[16, 12]])
    iota(("R4", 0, 4), [[1, 4]])
    do("g", lambda: g.affine_select(T.dg[:], T.half[:], [[-1, 128]], op_.is_equal, 0.0, 0, 1), [("half", 0, 128)], [("dg", 0, 128)])
    iota(("uoI", 0, 8), [[16, 8]])
    iota(("I4", 0, NT), [[0, NT // 4], [1, 4]])
    fill(("ZE", 0, 516), 0.0)
    act(("ZE", 3, 515, 4), ("dg", 0, 128))
    iota(("IO4", 0, NT + 2 * NC), [[4, NT + 2 * NC]])
    iota(("ad1", 0, NT), [[4, NT]])
    iota(("VW", XW + 4 * NC, GAP), [[0, GAP - XW - 4 * NC]])
    iota(("VW", GAP + XW + 4 * NC, WIN), [[0, 4 * NC]])
    iota(("ad2", 0, NT), [[4, NT]])
    ts(("pj", 0, 1), ("pi", 0, 1), 15, None, op_.bitwise_and)
    ts(("pj", 1, 2), ("pi", 0, 1), 15, 2, op_.bitwise_and, op_.logical_shift_right)
    ts(("pj", 2, 3), ("pi", 0, 1), 3, None, op_.bitwise_and)
    copy(("pf", 0, 3), ("pj", 0, 3))
    QP, RP, TP = ("pf", 0, 1), ("pf", 1, 2), ("pf", 2, 3)
    ts(("c16", 0, 12), ("K16", 0, 12), QP, None, op_.add)
    ts(("cm", 0, 4), ("R4", 0, 4), RP, None, op_.is_equal)
    ts(("nb", 0, 12), ("c16", 0, 12), -BIG, None, op_.mult)
    copy(("uo", 0, 8), ("uoI", 0, 8))
    ts(("cs", 0, 4), ("cm", 0, 4), 1.0 / GAP, None, op_.mult)
    ts(("cn", 0, 4), ("R4", 0, 4), RP, BIG, op_.not_equal, op_.mult)
    ts(("d16", 0, 12), ("c16", 0, 12), float(NT), None, op_.add)
    fill(("A1", 4 * NC, 512), 0.0)
    fill(("SC", 0, 4), 0.0)
    fill(("kb", 4 * NC, 512), 0.0)
    copy(("pt16", 0, 24), ("ptI", 0, 24))
    pick(("P1", 0, NT), ("IW", 0, NC), ("pt16", 0, 24))

    def pen_v(pen, row, k):
        ts((pen, k * NT, (k + 1) * NT), (row, 0, NT), ("c16", k, k + 1), BIG, op_.not_equal, op_.mult)

    def pen_s(pen, row, k):
        act((pen, k * NT, (k + 1) * NT), (row, 0, NT), AF.Abs, BIG, ("nb", k, k + 1))

    def to_list(out, row, col):
        for r in range(4):
            act((out, r, NT, 4), (row, r, NT, 4), scale=(col, r, r + 1))

    to_list("PM", "P1", "cm")
    quant("u", 0, 128, ("ub", 0, 512))
    do("v", lambda: V.tensor_copy(T.qur[:, 0:128].bitcast(dt.uint32), T.qu[:, 0:128].bitcast(dt.uint32).indirect(T.uo[:, 0:8])),
       [("qu", 0, 128), ("uo", 0, 8)], [("qur", 0, 128)])
    act(("sur", 0, 128), ("su", 0, 128), off=("uo", 0, 8))
    pen_v("pen1", "P1", 0)
    pen_v("pen1", "P1", 1)
    for k in range(PEN_S[0], 6):
        pen_s("pen1", "P1", k)
    ts(("r4", 0, NT), ("I4", 0, NT), 0.0, None, op_.not_equal)
    scan(("PS", 0, NT), ("r4", 0, NT), ("PM", 0, NT), 0.0, op_.mult, op_.add)
    ts(("L41", 0, NC), ("PS", 3, NT, 4), 4.0, TP, op_.mult, op_.add)
    copy(("ea2", 12, 18), ("c16", 6, 12))
    quant("xk", 0, NT, ("xb", 0, XW))
    mm(4, "ur", 0, "xk", 0, NT)
    for b in range(4):
        quant("E", 128 * b, 128 * b + 128, ("ZE", 3 - b, 515 - b))
    for b in range(4):
        mm(b, "E", 128 * b, "xk", 0, NT)

    for rnd in (0, 1):
        M = NC << rnd
        K = M // 16
        PL = NT + M
        row, pen, cma = ("P1", "pen1", "cma") if rnd == 0 else ("P2", "pen2", "cma2")
        ix, ea, qp, qb = ("ix1", "ea1", "qp1", "QB1") if rnd == 0 else ("ix2", "ea2", "qp2", "QB2")
        FG, A, AD, L4 = ("FG1", "A1", "ad1", "L41") if rnd == 0 else ("FG2", "AB", "ad2", "L42")
        B = ("B1", 0, 4 * M) if rnd == 0 else ("AB", 4 * M, 8 * M)
        h0 = 12 * rnd

        def gc(t):
            return ("GC1", t * NC, (t + 1) * NC) if rnd == 0 else ("GC2", t, 4 * M, 4)

        if rnd == 1:
            for t in range(4):
                act(("FG2", t * PL + NT, t * PL + PL), gc(t))
            for k in range(PEN_S[1], K):
                pen_s(pen, row, k)
        fb = list(range(4))

        def evac():
            b = fb.pop(0)
            act((FG, b * PL, b * PL + NT), bank(b, NT))

        def cells(b):
            pb = 5 + b % 3
            mm(pb, "E", 128 * b, "xk", NT, NT + 128)
            act((FG, b * PL + NT, b * PL + PL), bank(pb, NC))
            act(gc(b), bank(pb, NC))

        if rnd == 0:
            evac()
            evac()
        for k in range(K + 1):
            if k < K:
                if rnd == 1 and k < PEN_S[1]:
                    pen_v(pen, row, k)
                tt(("W", k * NT, (k + 1) * NT), bank(4, NT), (pen, k * NT, (k + 1) * NT), op_.subtract)
            if rnd == 0 and k == 0:
                quant("xk", NT, NT + 128, ("kb", 0, 512))
            if rnd == 0 and k == 5:
                copy(("ea1", 6, 12), ("adI", 0, 6))
            if k > 0:
                j = k - 1
                w, m = ("W", j * NT, k * NT), ("MX", j * NT, k * NT)
                scan(m, w, w, -2.0 ** 80, op_.max, op_.max)
                act(("JK", j * NT, k * NT), m, AF.Sign, -1.0, ("MX", k * NT - 1, k * NT), (ix, j, k))
                if fb and j >= 4 * rnd:
                    evac()
                elif rnd == 0 and j in (2, 3):
                    cells(2 * (j - 2))
                    cells(2 * (j - 2) + 1)
        H, QL, BL = ("hh", h0, h0 + K), (qb, 0, K), (qb, K, 2 * K)
        ts(H, ("MX", NT - 1, K * NT, NT), -2.0 ** 75, None, op_.is_le)
        if rnd == 0:
            tt(("cma", 0, 6), ("c16", 0, 6), ("ea1", 6, 12), op_.subtract)
        tt((ea, 0, K), H, ("d16", 0, K), op_.mult)
        tt((ix, K, 2 * K), H, (cma, 0, K), op_.mult)
        if rnd == 1:
            copy(("L42", 0, NC), ("Lg", 0, NC))
        tt((qp, 0, 2 * K), (ix, 0, 2 * K), (ea, 0, 2 * K), op_.add)
        copy((qb, 0, 2 * K), (qp, 0, 2 * K))
        bc = NC - BC[rnd]
        for t in range(4):
            tt((A, t, 4 * M, 4), (FG, t * PL, t * PL + PL), gc(t), op_.add, QL)
        act(("Ag", 0, 16 * bc), (A, 0, 4 * M), scale=0.5, off=(L4, 0, bc))
        qa, ra = ("a1", "r1") if rnd == 0 else ("a2", "r2")
        nA = max(M, 128)
        quant(qa, 0, nA, (A, 0, 4 * nA))
        wait("g", [hist["q" + qa][-1][2]])
        arr = T.sem["arr%d" % (rnd + 1)]
        g.remote_dma(T["q" + ra][:, 0:nA].bitcast(dt.uint8), T["q" + qa][:, 0:nA].bitcast(dt.uint8), arr, T.sem.sent, pid, rid, mask)
        g.remote_dma(T["s" + ra][:, 0:nA], T["s" + qa][:, 0:nA], arr, T.sem.sent, pid, rid, mask)
        atok = ("arr%d" % (rnd + 1), 2 * n_eng, {})
        note(("q" + ra, 0, nA), True, atok, "g")
        note(("s" + ra, 0, nA), True, atok, "g")
        final[atok[0]] = atok
        for t in range(4):
            tt((B[0], B[1] + t, B[2], 4), (FG, t * PL + NT, t * PL + PL), gc(t), op_.add, BL)
        act(("Bg", 0, XW), B, scale=0.5, off=(L4, 0, NC))
        ts(("Ag", 16 * bc, XW), (A, 0, 4 * M), 0.5, None, op_.mult, off=(L4, bc, NC))
        put((AD, 0, PL), ("IO4", NT, PL), QL)
        to_list("AM", AD, "cs")
        if rnd == 0:
            act(("P1m", 0, NT), ("P1", 0, NT), bias=-256.0)
        else:
            act(("P2m", 0, NT), ("P2", 0, NT), bias=-512.0)
        for b in range(4):
            tt(("VW", b, XW, 4), bank(b, NT), ("Ag", b, XW, 4), op_.add)
        quant("0%d" % (rnd + 1), 0, NT, ("VW", 0, XW))
        mm(5, "ur", 0, "0%d" % (rnd + 1), 0, NT)
        for r in range(4):
            act(("Z0", r, NT, 4), bank(5, NT, r, 4), AF.Identity, bias=("cn", r, r + 1))
        act(("Zc", 0, NT), bank(5, NT))
        for b in range(4):
            tt(("VW", GAP + b, GAP + XW, 4), bank(b, NT), ("Bg", b, XW, 4), op_.add)
        if rnd == 1:
            quant("v", 0, 128, ("vb", 0, 512))
        quant("1%d" % (rnd + 1), 0, NT, ("VW", GAP, GAP + XW))
        for b in range(4):
            pb = 7 if b % 2 == 0 else 4
            mm(pb, "w", 128 * b, ra, 0, nA)
            act(("VW", XW + b, XW + 4 * M, 4), bank(pb, M), scale=0.03125)
            if b == 1:
                mm(6, "ur", 0, "1%d" % (rnd + 1), 0, NT)
        act(("VW", GAP + XW, GAP + XW + 4 * M), ("VW", XW, XW + 4 * M))
        if rnd == 0:
            copy(("ea2", 18, 24), ("ea1", 6, 12))
            ts(("Lf", 0, NC), ("PS", 3, NT, 4), 4.0, TP, op_.mult, op_.add)
            tt(("cma2", 0, 12), ("c16", 0, 12), ("ea2", 12, 24), op_.subtract)
            act(("GC2", 0, 4 * NC), ("A1", 0, 4 * NC), scale=0.5)
            act(("GC2", 4 * NC, 8 * NC), ("B1", 0, 4 * NC), scale=0.5)
        else:
            quant("b", 0, M, B)
            mm(0, "v", 0, qa, 0, M)
            mm(1, "v", 0, "b", 0, M)
            act(("zb", 0, M), bank(0, M))
            act(("zb", M, 2 * M), bank(1, M))
            store("y", "z", T.z[:], T.zb[:], ("zb", 0, NT))
        tt(("CM", 0, NT), bank(6, NT), ("Z0", 0, NT), op_.is_gt)
        scan(("SC", 4, NT + 4), ("CM", 0, NT), ("AM", 0, NT), 0.0, op_.add, op_.add)
        tt(("T1", 0, NC), ("SC", 7, NT + 4, 4), ("SC", 3, NT, 4), op_.subtract)
        ts(("EL", 0, NC), ("T1", 0, NC), float(GAP), TP, op_.mult, op_.add)
        X, qx = ("X2", "x2") if rnd == 0 else ("X3", "x3")
        hc, c, cut, cut2 = NC // 2, NT // 2, CUT[rnd], CUT2[rnd]
        act((X, 16 * cut, 16 * hc), ("VW", 0, WIN), off=("EL", cut, hc))
        act((X, 16 * cut2, XW), ("VW", 0, WIN), off=("EL", cut2, NC))
        pick((X, 0, 16 * cut), ("VW", 0, WIN), ("EL", 0, cut))
        pick((X, 16 * hc, 16 * cut2), ("VW", 0, WIN), ("EL", hc, cut2))
        quant(qx, 0, c, (X, 0, 4 * c))
        tt(("CR", 0, NT), bank(6, NT), ("Zc", 0, NT), op_.is_gt)
        if rnd == 1:
            mm(7, "v", 0, qx, 0, c)
            store("y", "oc", T.oc[:, 0:4 * c], T.qx3[:, 0:c].bitcast(dt.uint8), ("qx3", 0, c))
            quant(qx, c, NT, (X, 4 * c, XW))
            mm(4, "v", 0, qx, c, NT)
        ts(("CS", 0, NT), ("CR", 0, NT), float(M), 256.0 if rnd == 0 else 512.0, op_.mult, op_.add)
        if rnd == 0:
            scan(("P2", 0, NT), ("CS", 0, NT), ("P1m", 0, NT), 0.0, op_.max, op_.add)
            quant(qx, c, NT, (X, 4 * c, XW))
            mm(4, "ur", 0, qx, 0, NT)
            for b in range(4):
                mm(b, "E", 128 * b, qx, 0, NT)
            ts(("Lt", 0, NC), ("T1", 0, NC), 1.0, 4.0 * M, op_.is_ge, op_.mult)
            tt(("Lg", 0, NC), ("Lt", 0, NC), ("Lf", 0, NC), op_.add)
        else:
            copy(("yb", 0, c), bank(7, c))
            store("y", "y0", T.y[:, 0:c], T.yb[:, 0:c], ("yb", 0, c))
            act(("yb", c, NT), bank(4, NT - c))
            store("s", "y1", T.y[:, c:NT], T.yb[:, c:NT], ("yb", c, NT))
            store("y", "oc1", T.oc[:, 4 * c:4 * NT], T.qx3[:, c:NT].bitcast(dt.uint8), ("qx3", c, NT))
            scan(("opr", 0, NT), ("CS", 0, NT), ("P2m", 0, NT), 0.0, op_.max, op_.add)
            for i in range(4):
                store("y", "o%d" % i, T.osc[4 * i:4 * i + 4, 0:NT], T.sx3[32 * i:32 * i + 4, 0:NT], ("sx3", 0, NT))
            store("y", "op", T.op[:], T.opr[0:128:16, 0:NT], ("opr", 0, NT))
    g.wait_ge(T.sem.sent, 4 * n_eng)
    wait("y", list(final.values()))
